import numpy as np, ml_dtypes
CORES = [9,25,41,57]
N = 4
BF = ml_dtypes.bfloat16
def gentries(a):
    return np.ascontiguousarray(a.reshape(8, 16, -1).transpose(0, 2, 1)).reshape(8, -1)
def gtable(e):
    e = np.asarray(e); return np.ascontiguousarray(e.reshape(8, -1, 16).transpose(0, 2, 1)).reshape(128, -1).astype(np.int32)
W, M, B, T, P, QU, TH = 4096, 1024, 256, 4, 2, 12, 254
def parts(rng):
    d = {}
    d["pr"] = (224 * rng.random((N, 8, 1, W)) ** 3 + 32 * rng.random((N, 8, 16, W))).astype(np.int64)
    d["ad"] = (np.exp2(rng.integers(2, 8, (N, 8, 1, W))) * rng.random((N, 8, 16, W))).astype(np.int64)
    d["mc"] = rng.integers(0, W, (N, 8, 16, M))
    d["gl"] = (224 * rng.random((N, 8, 1, M)) + 32 * rng.random((N, 8, 16, M))).astype(np.int64)
    d["z"] = (224 * rng.random((N, 8, 1, B)) + 32 * rng.random((N, 8, 16, B))).astype(np.int64)
    d["m"] = rng.integers(0, M, (N, 8, B))
    d["dv"] = (np.exp2(rng.integers(2, 8, (N, 8, 1, T * P))) * rng.random((N, 8, 16, T * P))).astype(np.int64)
    d["wt"] = rng.integers(0, 256, (N, 8, 16, 1))
    return d
def flat(a):
    return np.ascontiguousarray(np.reshape(a, (N, 128, -1)))
def pack(d):
    h = {k: flat(d[k]).astype(np.float32).astype(BF) for k in ("pr", "ad", "gl", "z", "dv", "wt")}
    return {"pr": h["pr"], "ad": h["ad"], "mc": flat(d["mc"]).astype(np.int32), "gl": h["gl"], "z0": h["z"], "m0": np.stack([gtable(a) for a in d["m"]]), "dv": h["dv"], "wt": h["wt"]}
def setup_inputs(rng):
    return pack(parts(rng))
def sized(rng, hi, *shape):
    return np.minimum((float(hi + 1) ** rng.random(shape[:-2] + (1, shape[-1])) * rng.random(shape)).astype(np.int64), hi)
def setup_inputs_spread(rng):
    d = parts(rng)
    d["pr"] = sized(rng, 255, N, 8, 16, W); d["ad"] = sized(rng, 127, N, 8, 16, W); d["dv"] = sized(rng, 255, N, 8, 16, T * P); d["wt"] = sized(rng, 255, N, 8, 16, 1)
    a = sized(rng, 255, N, 8, 16, M); d["gl"] = np.where(rng.random((N, 8, 1, M)) < 0.5, 255 - a, a)
    a = sized(rng, 255, N, 8, 16, B); d["z"] = np.where(rng.random((N, 8, 1, B)) < 0.6, rng.integers(0, 256, (N, 8, 16, B)), a)
    d["mc"] = np.minimum((W * rng.random((N, 8, 16, M)) ** 3).astype(np.int64), W - 1)
    d["m"] = np.minimum((M * rng.random((N, 8, B)) ** 2).astype(np.int64), M - 1)
    return pack(d)
def mix(rng, hi, *shape):
    q = rng.choice(np.array([0.0, 0.1, 0.5, 0.8, 0.9, 1.0]), shape[:-2] + (1, shape[-1]))
    return (rng.random(shape) < q).astype(np.int64) * hi
def setup_inputs_ends(rng):
    d = {"pr": mix(rng, 255, N, 8, 16, W), "ad": mix(rng, 127, N, 8, 16, W), "mc": mix(rng, W - 1, N, 8, 16, M), "gl": mix(rng, 255, N, 8, 16, M), "z": mix(rng, 255, N, 8, 16, B),
         "m": (M - 1) * rng.integers(0, 2, (N, 8, B)), "dv": mix(rng, 255, N, 8, 16, T * P), "wt": mix(rng, 255, N, 8, 16, 1)}
    pr, ad, mc, gl, z, m, dv, wt = [d[k] for k in ("pr", "ad", "mc", "gl", "z", "m", "dv", "wt")]; a = N - 1
    wt[:, 0, :8] = 0; wt[:, 0, 8:] = 255
    gl[0, :, :, 0] = 0; gl[0, :, :, M - 1] = 0
    gl[1, :, :, 0] = 0; gl[1, :, :, M - 1] = 255; m[1] = 0; m[1, 7, B - 1] = M - 1; z[1, 7, :, B - 1] = 0; dv[1, 7, :, :P] = 0
    pr[a, 7, :, 0] = 255; ad[a, 7, :, 0] = 127; ad[a, 7, :, W - 1] = 0; gl[a, 7, :, 0] = 255; gl[a, 7, :, M - 1] = 255
    mc[a, 7, :, 0] = 0; mc[a, 7, :, M - 1] = W - 1
    wt[a, 7] = 0; wt[a, 7, 15] = 255; wt[a, 7, 13:15] = 1
    for i in (0, 1, B - 2, B - 1): z[a, 7, :, i] = 255
    m[a, 7, 1] = 0; m[a, 7, B - 2] = 0; m[a, 7, B - 1] = M - 1
    m[a, 7, :B - 1] = np.where(np.all(z[a, 7, 13:, :B - 1] == 255, axis=0), 0, m[a, 7, :B - 1])
    wt[a, 6] = 255; gl[a, 6, :, 0] = 0; z[a, 6, :, 0] = 255; z[a, 6, :, B - 1] = 255; z[a, 6, :, 1] = 0; z[a, 6, :, B - 2] = 0
    m[a, 6, 0] = 0; m[a, 6, 1] = 0; m[a, 6, B - 2] = 0; m[a, 6, B - 1] = M - 1
    return pack(d)
def setup_inputs_corners(rng):
    d = parts(rng); pr, ad, mc, gl, z, m, dv, wt = [d[k] for k in ("pr", "ad", "mc", "gl", "z", "m", "dv", "wt")]
    m[:, 0] = 0; m[:, 1] = M - 1; m[:, 2] = np.arange(B); m[:, 3] = M - 1 - np.arange(B)
    wt[:, 0] = 0; wt[:, 1] = 255; dv[:, 4] = 255; dv[:, 5] = 0
    one = rng.integers(0, W, (N, 1, M)); one[:, 0, 0] = 0; one[:, 0, M - 1] = W - 1; mc[:, 4] = one; m[:, 4, 0] = 0; m[:, 4, B - 1] = M - 1
    gl[:, 5] = np.maximum(gl[:, 5], 1); goal = np.take_along_axis(gl[:, 5], m[:, 5][:, None, :], 2)
    c = rng.choice(np.array([0, QU - 1, QU, QU + 1, 16]), (N, 1, B)); place = np.argsort(np.argsort(rng.random((N, 16, B)), axis=1), axis=1)
    z[:, 5] = goal - (place >= c)
    ad[:, 6] = TH // 16; ad[:, 6, 15] = TH - 15 * (TH // 16) + rng.integers(-1, 2, (N, W))
    pr[:, 6] = np.maximum(pr[:, 6], 40); gl[:, 6] = np.maximum(gl[:, 6], 200); z[:, 6] = np.where(rng.random((N, 1, B)) < 0.7, 255, z[:, 6])
    pr[:, 7] = 255; gl[:, 7] = 255; z[:, 7] = 255 * rng.integers(0, 2, (N, 1, B)); wt[:, 7] = (255 * (np.arange(N) & 1)).reshape(N, 1, 1)
    return pack(d)
def setup_inputs_crowd(rng):
    d = parts(rng); pr, gl, z, m, dv, wt = [d[k] for k in ("pr", "gl", "z", "m", "dv", "wt")]
    gl[:, :6] = 0; m[:, :4] = np.argsort(rng.random((N, 4, M)), axis=-1)[..., :B]
    wt[:, :4] = 0; wt[:, :4, 0] = 1; wt[:, :4, 1] = 255
    c = np.full((N, 4, B), M - 1); c[:, 1, 0] = 0; c[:, 3] = rng.choice(np.array([0, 1, M // 2, M - 1]), (N, B))
    v = (c - 37 * m[:, :4]) & (M - 1); z[:, :4, 0] = v - 255 * (v // 255); z[:, :4, 1] = v // 255
    for i in range(N): gl[i, 2, :, m[i, 2, 0]] = 255
    z[:, 2, 2:, 0] = 100; dv[:, 2, :, :P] = 1
    for g in (4, 5):
        z[:, g] = z[:, g, :, :1].copy(); m[:, g] = m[:, g, :1].copy()
    z[:, 5, :, B - 1] = 255 - z[:, 5, :, 0]
    gl[:, 6] = 255
    pr[:, 7] = 255; gl[:, 7] = 255; z[:, 7] = 0; z[:, 7, :, B - 1] = 255; m[:, 7] = m[:, 7, :1].copy()
    return pack(d)
def setup_inputs_few(rng):
    d = parts(rng); d["z"] = np.minimum(d["z"], 254); d["dv"] = np.maximum(d["dv"], 1)
    mc, gl, z, m, wt = [d[k] for k in ("mc", "gl", "z", "m", "wt")]
    gl[1::2] = 255; z[1::2, 7, :, B - 1] = 255
    full = rng.permutation(np.array([0, 1, 3, 4]))
    for i in range(0, N, 2):
        g = int(full[(i // 2) & 3]); gl[i, g] = 0; m[i, g] = rng.permutation(M)[:B]
        wt[i, g] = 0; wt[i, g, 0] = 1; wt[i, g, 1] = 255
        a = rng.choice(np.array([11, 13, 23, 25, 27, 29]), B); u = W - 32 + a
        z[i, g, 1] = u // 255; z[i, g, 0] = u - 255 * (u // 255)
        mc[i, g, 15, m[i, g]] = W - 32 + ((-(a ** 7)) & 31)
    return pack(d)
def check_inputs(d):
    bad = []
    for k, hi in (("pr", 255), ("ad", 127), ("mc", W - 1), ("gl", 255), ("z0", 255), ("m0", M - 1), ("dv", 255), ("wt", 255)):
        a = np.asarray(d[k]).astype(np.float64)
        if not (np.min(a) >= 0 and np.max(a) <= hi): bad.append("range of " + k)
        elif np.any(a != np.floor(a)): bad.append("whole numbers of " + k)
    return bad
def reference(pr, ad, mc, gl, z0, m0, dv, wt):
    need_of, add_of, goal_of, z, dist, weight = [a.astype(np.float32).astype(np.int64).reshape(N, 8, 16, -1) for a in (pr, ad, gl, z0, dv, wt)]
    tb = mc.astype(np.int64).reshape(N, 8, 16, M); m = np.stack([gentries(a) for a in m0]).astype(np.int64)
    seen = [0] * N
    for t in range(T):
        for q in range(N):
            s = (q - t) % N; zz = z[s]; mm = m[s]
            o = np.take_along_axis(tb[q], mm[:, None, :], 2)
            ix = o.reshape(8, 1, 16 * B)
            p = np.take_along_axis(need_of[q], ix, 2).reshape(8, 16, 16, B); a = np.take_along_axis(add_of[q], ix, 2).reshape(8, 16, 16, B)
            K = [None] * 16 + [np.take_along_axis(goal_of[q], mm[:, None, :], 2)]
            for k in range(15, -1, -1): K[k] = np.maximum(p[:, :, k], K[k + 1] - a[:, :, k])
            K = np.stack(K)
            for j in range(P):
                met = np.add.reduce((zz[None] >= K).astype(np.int64), axis=2)
                best = np.max(np.where(met >= QU + (seen[q] & 1), np.arange(17).reshape(17, 1, 1), -1), axis=0)
                ak = np.take_along_axis(a, np.clip(best, 0, 15)[:, None, None, :], 2)[:, :, 0]
                new = np.abs(np.minimum(255, zz + ak) - dist[q, :, :, t * P + j][:, :, None])
                zz = np.where(((best >= 0) & (best < 16))[:, None, :], new, zz)
            goal = best == 16
            u = np.add.reduce(weight[q] * zz, axis=1) & (W - 1); to = (u + 37 * mm) & (M - 1)
            use = np.add.reduce(np.minimum(a, K[1:].transpose(1, 2, 0, 3)), axis=1)
            fresh = (((o * u[:, None, :]) >> 5) + o + 37 * np.arange(16).reshape(1, 16, 1)) & (W - 1)
            o = np.where(use < TH, fresh, o)
            for g in range(8):
                who = np.flatnonzero(goal[g]); where, first = np.unique(to[g, who], return_index=True)
                tb[q, g][:, where] = o[g][:, who[first]]
            z[s] = zz; m[s] = np.where(goal | (best < 0), to, mm); seen[q] = int(np.count_nonzero(goal))
    back = [(q - (T - 1)) % N for q in range(N)]
    return {"ymc": tb.reshape(N, 128, M).astype(np.float32), "yz": z[back].reshape(N, 128, B).astype(np.float32), "ym": np.stack([gtable(m[s]) for s in back]).astype(np.float32)}

@@ -1,0 +1,387 @@
+from concourse.mybir import dt, AluOpType as OP, AxisListType, ActivationFunctionType as AF
+
+F, H, I, U = "float32", "bfloat16", "int32", "uint16"
+SB = {
+    "MC": (1280, I), "MCF": (1280, F), "PR": (4096, H), "AD": (4096, H), "GL": (1024, H), "M0": (16, I),
+    "DV": (8, H), "WT": (1, H), "DH": (8, F), "DG": (1024, H), "OU": (256, U), "OF": (256, F), "Z": (256, H), "ZF": (256, F),
+    "KV": (144, F), "BASE": (8, F), "IOTA": (4096, F), "BT": (1280, H), "BTI": (1280, I), "YB": (256, H),
+    "ON": (144, H), "IDN": (128, H), "NID": (128, H), "I128": (128, H), "BLK": (128, H), "BLB": (128, H), "CST": (128, H),
+    "RM": (2048, H), "RMN": (2048, H), "RMC": (2048, H), "RMW": (2048, H), "TH": (128, H), "MSK": (8, F),
+    "PI": (1, I), "PR16": (1, I), "R16": (1, F), "R32": (1, F), "C37": (1, F), "PW": (1, F), "TM": (16, H), "GOB": (16, H),
+    "MI": (16, I), "MI2": (16, I), "MS": (16, U), "XU": (16, U), "UI": (16, I), "UI2": (16, I), "UU": (16, U), "XFU": (16, U),
+    "OG": (256, F), "PP": (256, I), "SS": (256, I), "TT": (256, I), "NW": (256, I), "JK": (256, H), "AC": (1, F), "AI": (1, I), "AP": (1, I), "AT": (1, F),
+}
+for _n in "I16 E16 PWR SX KD GO NN GN T36 BM MF CA CB UM YM XA X DM DVX DA DF XD XF".split(): SB[_n] = (16, F)
+for _h in "0123": SB["ZI" + _h], SB["MU" + _h] = (256, H), (16, U)
+for _h in "01":
+    for _n, _w, _d in (("G", 128, H), ("AB", 4112, H), ("PB", 4112, H), ("KB", 4096, H), ("KS", 144, F), ("KU", 8, U), ("VG", 128, H), ("SG", 128, H), ("T2", 128, H), ("R0", 128, H)):
+        SB[_n + _h] = (_w, _d)
+SCRATCH = {k: ("sbuf", [128, w], d) for k, (w, d) in SB.items()}
+for _h in "01":
+    SCRATCH["C" + _h] = ("sbuf", [128, 8, 16, 18], H)
+    SCRATCH["BR" + _h] = ("sbuf", [128, 8, 18], H)
+SCRATCH["BD"] = ("sbuf", [128, 16, 8, 16], H)
+for _b in range(8):
+    SCRATCH["P%d" % _b] = ("psum", [128, 512], F)
+LOADS = {"m0": 2.2, "mc": 4.5, "gl": 6, "z0": 6.5, "pr": 9, "ad": 9, "dv": 3, "wt": 3}
+SEMAPHORES = ["sV", "sA", "sT", "sG", "so0", "so1", "so2"] + ["ld_" + n for n in LOADS] + ["%s%d" % (n, t) for n in ("zi", "mi", "zl", "ml") for t in range(1, 4)]
+
+CYC, WAKE, CG, PF = 0.00104, 0.12, 1.56, 0.5
+NA, EPS = 6, 0.1
+
+
+def build(T, topo, core, nxt):
+    ops, wr, rd, bk = [], {}, {}, {}
+
+    def op(eng, fn, reads, writes, cost, banks=(), done=None):
+        i = len(ops)
+        hard, soft = set(), set()
+        for k in reads:
+            if k in wr: hard.add(wr[k])
+        for k in writes:
+            if k in wr: hard.add(wr[k])
+            for r in rd.get(k, ()):
+                if r != i: (soft if ops[r]["eng"] == eng and eng in "VATGS" and ops[r]["done"] is None else hard).add(r)
+        for b in banks:
+            for r in bk.setdefault(b, []):
+                if ops[r]["eng"] != eng: hard.add(r)
+            bk[b].append(i)
+        for k in reads: rd.setdefault(k, []).append(i)
+        for k in writes:
+            wr[k] = i
+            rd[k] = []
+        ops.append({"eng": eng, "fn": fn, "hard": hard, "soft": soft - hard, "cost": cost, "done": done, "w": writes})
+
+    def V(fn, reads, writes, n, banks=(), f=1.0):
+        op("V", fn, reads, writes, max(64, n * f) * CYC + 0.02, banks)
+
+    def G(fn, reads, writes, cost):
+        op("G", fn, reads, writes, cost)
+
+    def copy(o, i, r, w, n, banks=(), f=1.0):
+        V(lambda q: q.tensor_copy(o, i), r, w, n, banks, f)
+
+    def ts(o, i, s1, o1, s2, o2, r, w, n, banks=(), f=1.0):
+        if o2 is None: V(lambda q: q.tensor_scalar(o, i, s1, None, o1), r, w, n, banks, f)
+        else: V(lambda q: q.tensor_scalar(o, i, s1, s2, o1, o2), r, w, n, banks, f)
+
+    def tt(o, a, b, f, r, w, n, banks=(), c=2.0):
+        V(lambda q: q.tensor_tensor(o, a, b, f), r, w, n, banks, c)
+
+    def act(o, i, func, r, w, n, banks=(), gather=False, **kw):
+        op("A", lambda q: q.activation(o, i, func, **kw), r, w, 0.08 + n * CG * CYC if gather else max(64, n) * CYC + 0.05, banks)
+
+    def gath(o, i, neg, r, w, n):
+        def fn(q, e):
+            if e == "A": return q.activation(o, i, AF.Copy, scale=-1.0 if neg else 1.0)
+            return q.tensor_scalar(o, i, -1.0, None, OP.mult) if neg else q.tensor_copy(o, i)
+        op("VA", fn, r, w, 0.08 + n * CG * CYC)
+
+    def fill(o, c, w, n):
+        V(lambda q: q.memset(o, c), [], [w], n, (), 0.5)
+
+    def mm(lst, r, w, n, banks):
+        def fn(q):
+            x = None
+            for (o, l, rr, s, e) in lst: x = q.matmul(o, l, rr, s, e)
+            return x
+        op("T", fn, r, w, n * CYC * PF + 0.05, banks)
+
+    def load(q, name, dst, key):
+        op(q, lambda e: e.dma_start(dst, T[name][:]), [], [key], 0.1, (), ("ld_" + name, 16, LOADS[name]))
+
+    load("S", "m0", T.M0[:], "M0"); load("S", "mc", T.MC[:, 0:1024], "MC"); load("S", "pr", T.PR[:], "PR"); load("S", "z0", T.ZI0[:], "ZI0")
+    load("A", "wt", T.WT[:], "WT"); load("A", "dv", T.DV[:], "DV"); load("A", "ad", T.AD[:], "AD"); load("A", "gl", T.GL[:], "GL")
+    fill(T.ON[:], 1.0, "ON", 144)
+    fill(T.RM[:], 1.0, "RM", 2048)
+    RM, imp = T.RM[:], {"allow_small_or_imprecise_dtypes": True}
+    G(lambda q: q.iota(T.PI[:], [[0, 1]], 0, 1), [], ["PI"], 0.2)
+    G(lambda q: q.iota(T.I16[:], [[1, 16]], 0, 0, **imp), [], ["I16"], 0.2)
+    G(lambda q: q.affine_select(T.IDN[:], T.ON[:, 0:128], [[-1, 128]], OP.is_equal, 0.0, 0, 1), ["ON"], ["IDN"], 0.5)
+    G(lambda q: q.affine_select(T.BLB[:], T.ON[:, 0:128], [[-16, 8], [0, 16]], OP.is_ge, 0.0, 0, 1), ["ON"], ["BLB"], 0.5)
+    G(lambda q: q.affine_select(T.BLK[:], T.BLB[:], [[16, 8], [0, 16]], OP.is_ge, 0.0, 15, -1), ["BLB"], ["BLK"], 0.5)
+    G(lambda q: q.iota(T.KV[:], [[512, 8], [2, 18]], 14, 0, **imp), [], ["KV"], 0.5)
+    G(lambda q: q.iota(T.SX[:], [[16, 16]], 1024, 0, **imp), [], ["SX"], 0.2)
+    G(lambda q: q.affine_select(RM, RM, [[-1, 16], [0, 8], [1, 16]], OP.is_equal, 0.0, 0, 0), ["RM"], ["RM"], 4.0)
+    G(lambda q: q.affine_select(RM, RM, [[0, 16], [-16, 8], [0, 16]], OP.is_ge, 0.0, 0, 1), ["RM"], ["RM"], 4.0)
+    G(lambda q: q.affine_select(RM, RM, [[0, 16], [16, 8], [0, 16]], OP.is_ge, 0.0, 15, -1), ["RM"], ["RM"], 4.0)
+    G(lambda q: q.iota(T.IOTA[:], [[1, 4096]], 0, 0, **imp), [], ["IOTA"], 8.0)
+    for h in range(2):
+        AB, PB = T["AB%d" % h], T["PB%d" % h]
+        fill(AB[:, 15:4112:2], 0.0, "ABo%d" % h, 2049)
+        fill(AB[:, 15:4112:32], -256.0, "ABo%d" % h, 129)
+        fill(PB[:, 18:4112:2], 0.0, "PBz%d" % h, 2047)
+        fill(T["C%d" % h][:, :, :, 0], 1.0, ("C", h, 0), 128)
+    fill(T.BR0[:, :, 0:18 - NA], 1.0, ("BR", 0), 144)
+    fill(T.BR0[:, :, 18 - NA:18], 2.0, ("BR", 1), 144)
+    fill(T.BR1[:, :, 0:18 - NA], 0.0, ("BR", 2), 144)
+    fill(T.BR1[:, :, 18 - NA:18], 1.0, ("BR", 3), 144)
+    fill(T.CST[:], 2048.0, "CST", 128)
+    fill(T.TH[:], -1472.0, "TH", 128)
+    ts(T.PR16[:], T.PI[:], 15, OP.bitwise_and, None, None, ["PI"], ["PR16"], 1)
+    copy(T.R16[:], T.PR16[:], ["PR16"], ["R16"], 1)
+    ts(T.R32[:], T.R16[:], 32.0, OP.mult, None, None, ["R16"], ["R32"], 1)
+    ts(T.C37[:], T.R16[:], 37.0, OP.mult, None, None, ["R16"], ["C37"], 1)
+    ts(T.KV[:], T.KV[:], T.R32[:, 0:1], OP.add, None, None, ["R32", "KV"], ["KV"], 144)
+    ts(T.KV[:, 0:144:18], T.KV[:, 0:144:18], 1.0, OP.add, None, None, ["KV"], ["KV"], 8)
+    ts(T.KV[:, 17:144:18], T.KV[:, 17:144:18], -1.0, OP.add, None, None, ["KV"], ["KV"], 8)
+    ts(T.BASE[:], T.KV[:, 0:144:18], 1.0, OP.add, None, None, ["KV"], ["BASE"], 8)
+    ts(T.SX[:], T.SX[:], T.R16[:, 0:1], OP.add, None, None, ["R16", "SX"], ["SX"], 16)
+    ts(T.E16[:], T.I16[:], T.R16[:, 0:1], OP.is_equal, None, None, ["R16", "I16"], ["E16"], 16)
+    ts(T.TM[:], T.I16[:], T.R16[:, 0:1], OP.is_ge, -64.0, OP.mult, ["R16", "I16"], ["TM"], 16)
+    for b in range(16): fill(T.PWR[:, b:b + 1], 2.0 ** -b, ("PWR", b), 1)
+    tt(T.E16[:], T.E16[:], T.PWR[:], OP.mult, ["E16"] + [("PWR", b) for b in range(16)], ["E16"], 16)
+    V(lambda q: q.tensor_reduce(T.PW[:], T.E16[:], AxisListType.X, OP.add), ["E16"], ["PW"], 16)
+    ts(T.BTI[:], T.IOTA[:, 0:1280], T.PW[:, 0:1], OP.mult, -0.5 + 2.0 ** -13, OP.add, ["IOTA", "PW"], ["BTI"], 1280)
+    ts(T.BTI[:], T.BTI[:], 1, OP.bitwise_and, None, None, ["BTI"], ["BTI"], 1280)
+    ts(T.BT[:], T.BTI[:], 2.0, OP.mult, -1.0, OP.add, ["BTI"], ["BT"], 1280)
+    ts(T.NID[:], T.IDN[:], -1.0, OP.mult, None, None, ["IDN"], ["NID"], 128, (), 0.5)
+    ts(T.I128[:], T.IDN[:], 128.0, OP.mult, None, None, ["IDN"], ["I128"], 128, (), 0.5)
+    act(T.RMC[:], RM, AF.Copy, ["RM"], ["RMC"], 2048, scale=16384.0)
+    act(T.RMN[:], RM, AF.Copy, ["RM"], ["RMN"], 2048, scale=-1.0)
+    ts(T.RMW[:], RM, T.WT[:, 0:1], OP.mult, None, None, ["RM", "WT"], ["RMW"], 2048, (), 0.5)
+    copy(T.MSK[:], T.BLK[:, 0:128:16], ["BLK"], ["MSK"], 8)
+    ts(T.DH[:], T.DV[:], -0.5, OP.mult, None, None, ["DV"], ["DH"], 8)
+    for j in range(8):
+        ts(T.DG[:, 128 * j:128 * j + 128], T.IDN[:], T.DH[:, j:j + 1], OP.mult, None, None, ["IDN", "DH"], [("DG", j)], 128, (), 0.5)
+    copy(T.MU0[:], T.M0[:], ["M0"], ["MU0"], 16)
+
+    for t in range(4):
+        ZI, MU = T["ZI%d" % t], T["MU%d" % t]
+        zk, mk = "ZI%d" % t, "MU%d" % t
+        if t:
+            nw = 8
+            op("", None, [zk + "s"], [zk], 0, (), ("zi%d" % t, nw, 3.0))
+            op("", None, [mk + "s"], [mk], 0, (), ("mi%d" % t, nw, 3.0))
+        for h in range(2):
+            a = 128 * h
+            copy(T.OU[:, a:a + 128], T.MC[:, 0:1024].indirect(MU[:, 8 * h:8 * h + 8]), ["MC", mk], [("OU", h)], 128, (), CG)
+            act(T["G%d" % h][:], T.GL[:].indirect(MU[:, 8 * h:8 * h + 8]), AF.Copy, ["GL", mk], ["G%d" % h], 128, gather=True)
+        copy(T.MF[:], MU[:], [mk], ["MF"], 16)
+        for h in range(2):
+            Zb, Xb, Eb, Fb = T["P%d" % h], T["P%d" % (2 + h)], T["P%d" % (6 + h)], T["P%d" % (5 - h)]
+            AB, PB, KB, C = T["AB%d" % h], T["PB%d" % h], T["KB%d" % h], T["C%d" % h]
+            KS, KU, vg, sg, T2, R0, G_ = [T[n + str(h)] for n in ("KS", "KU", "VG", "SG", "T2", "R0", "G")]
+            a, b = 128 * h, 128 * h + 128
+            mm([(Zb[:, 0:128], T.IDN[:], ZI[:, a:b], True, True)], [zk, "IDN"], ["ZP%d" % h], 128, [h])
+            ch = 4
+            n = 128 // ch
+            for c in range(ch):
+                lo, s0 = 32 * n * c, a + n * c
+                gath(PB[:, 15 + lo:15 + lo + 32 * n:2], T.PR[:].indirect(T.OU[:, s0:s0 + n]), False, ["PR", ("OU", h)], [("PB", h, c)], 16 * n)
+                gath(AB[:, 16 + lo:16 + lo + 32 * n:2], T.AD[:].indirect(T.OU[:, s0:s0 + n]), True, ["AD", ("OU", h)], [("AB", h, c)], 16 * n)
+            pk, ak = [("PB", h, c) for c in range(ch)], [("AB", h, c) for c in range(ch)]
+            copy(PB[:, 16:4112:32], PB[:, 15:4111:32], pk + ["PBz%d" % h], ["P0%d" % h], 128, (), 0.5)
+            copy(PB[:, 47:4112:32], G_[:], ["G%d" % h, "P0%d" % h], pk, 128, (), 0.5)
+            V(lambda q, KB=KB, AB=AB, PB=PB: q.tensor_tensor_scan(KB[:, ::-1], AB[:, 4111:15:-1], PB[:, 4111:15:-1], 0.0, OP.add, OP.max),
+              pk + ak + ["P0%d" % h, "PBz%d" % h, "ABo%d" % h], ["KB%d" % h], 4096, (), 0.5)
+            mm([(Eb[:, 0:128], T.IDN[:], KB[:, 1:4096:32], True, False), (Eb[:, 0:128], T.IDN[:], AB[:, 16:4112:32], False, True)],
+               ["IDN", "KB%d" % h] + ak, ["E0%d" % h], 256, [6 + h])
+            act(R0[:], Eb[:, 0:128], AF.Relu, ["E0%d" % h], ["R0%d" % h], 128, [6 + h])
+            us, lst = Xb[:, 272:400], []
+            for k in range(16):
+                lst.append((us, T.RM[:, 128 * k:128 * k + 128], KB[:, 2 * k + 1:4096:32], k == 0, False))
+                lst.append((us, T.RMN[:, 128 * k:128 * k + 128], KB[:, 2 * k:4096:32] if k else R0[:], False, k == 15))
+            mm(lst, ["RM", "RMN", "KB%d" % h, "R0%d" % h], [("US", h)], 32 * 128, [2 + h])
+            zsrc, zkey = ZI[:, a:b], zk
+            kpos = [2 * k - 1 if k else 0 for k in range(17)]
+            for j in range(2):
+                for B, bank, ks in ((Eb, 6 + h, range(17 - NA, 17 - NA // 2)), (Fb, 5 - h, range(17 - NA // 2, 17))):
+                    lst = []
+                    for i, k in enumerate(ks):
+                        lst.append((B[:, 128 * i:128 * i + 128], T.IDN[:], zsrc, True, False))
+                        lst.append((B[:, 128 * i:128 * i + 128], T.NID[:], KB[:, kpos[k]:4096:32], False, True))
+                    mm(lst, ["IDN", "NID", zkey, "KB%d" % h], [("D", h, bank)], 128 * len(lst), [bank])
+                    for i, k in enumerate(ks):
+                        act(C[:, :, :, k + 1], B[:, 128 * i:128 * i + 128], AF.Sign, [("D", h, bank)], [("C", h, k + 1)], 128, [bank], bias=0.5)
+                for k in range(17 - NA):
+                    tt(C[:, :, :, k + 1], KB[:, kpos[k]:4096:32], Zb[:, 0:128], OP.is_le, ["KB%d" % h, "ZP%d" % h], [("C", h, k + 1)], 128, [h], 1.0)
+                cp = Xb[:, 0:144]
+                lst = [(cp, T.TH[:], T.BR0[:], True, False), (cp, T.CST[:], T.BR1[:], False, False)]
+                lst += [(cp, T.RMC[:, 128 * r:128 * r + 128], C[:, :, r, :], False, r == 15) for r in range(16)]
+                mm(lst, [("C", h, k) for k in range(18)] + [("BR", x) for x in range(4)] + ["RMC", "CST", "TH"], ["CP%d" % h], 18 * 144, [2 + h])
+                V(lambda q, KS=KS, cp=cp: q.tensor_tensor_scan(KS[:], cp, T.KV[:], 0.0, OP.max, OP.min), ["CP%d" % h, "KV"], ["KS%d" % h], 144, [2 + h])
+                copy(KU[:], KS[:, 17:144:18], ["KS%d" % h], ["KU%d" % h], 8)
+                abk = ak + ["ABo%d" % h, "KU%d" % h]
+                act(sg[:], AB[:].indirect(KU[:]), AF.Sign, abk, ["SG%d" % h], 128, gather=True, bias=192.0)
+                gath(vg[:], AB[:].indirect(KU[:]), False, abk, ["VG%d" % h], 128)
+                xs, dj = Xb[:, 144:272], 2 * t + j
+                mm([(xs, T.IDN[:], zsrc, True, False), (xs, T.NID[:], vg[:], False, False), (xs, T.I128[:], sg[:], False, True)],
+                   [zkey, "IDN", "NID", "I128", "VG%d" % h, "SG%d" % h], ["X1%d" % h], 384, [2 + h])
+                ts(T2[:], xs, 383.0, OP.min, 128.0, OP.subtract, ["X1%d" % h], ["T2%d" % h], 128, [2 + h])
+                mm([(xs, T.IDN[:], T2[:], True, False), (xs, T.DG[:, 128 * dj:128 * dj + 128], sg[:], False, True)],
+                   ["IDN", ("DG", dj), "T2%d" % h, "SG%d" % h], ["X1%d" % h], 256, [2 + h])
+                bias, xr = T.DH[:, dj:dj + 1], ["X1%d" % h, "DH"]
+                if j == 0: act(Zb[:, 0:128], xs, AF.Abs, xr, ["ZP%d" % h], 128, [h, 2 + h], bias=bias)
+                act(T.Z[:, a:b], xs, AF.Abs, xr, ["Z%d" % h], 128, [2 + h], bias=bias)
+                if t == 3 and j == 1: act(T.ZF[:, a:b], xs, AF.Abs, xr, ["ZF%d" % h], 128, [2 + h], bias=bias)
+                zsrc, zkey = T.Z[:, a:b], "Z%d" % h
+            ul = T.P6[:, 496 + 8 * h:504 + 8 * h]
+            mm([(ul, T.RMW[:, 128 * r:128 * r + 128], T.Z[:, a + r:b:16], r == 0, r == 15) for r in range(16)], ["RMW", "Z%d" % h], [("UL", h)], 1024, [6])
+            tt(T.KD[:, 8 * h:8 * h + 8], KS[:, 17:144:18], T.BASE[:], OP.subtract, ["KS%d" % h, "BASE"], [("KD", h)], 8)
+
+        def send(q, src, name, sem):
+            rid, pid, _ = topo.addr(nxt)
+            q.remote_dma(T[name][:], src[:], T.sem[sem % "i"], T.sem[sem % "l"], pid, rid, topo.mask(core, nxt))
+        n1 = t + 1
+        if t < 3:
+            op("G", lambda q, n1=n1: send(q, T.Z, "ZI%d" % n1, "z%%s%d" % n1), ["Z0", "Z1"], ["ZI%ds" % n1], 0.5, (), ("zl%d" % n1, 8, 2.0))
+        KDK, ULK = [("KD", 0), ("KD", 1)], [("UL", 0), ("UL", 1)]
+        copy(T.OF[:], T.OU[:], [("OU", 0), ("OU", 1)], ["OF"], 256)
+        for h in range(2):
+            us, a = T["P%d" % (2 + h)][:, 272:400], 128 * h
+            ts(T.P5[:, a:a + 128], us, 254.0, OP.is_lt, None, None, [("US", h)], [("GG", h)], 128, [5, 2 + h])
+            ts(T.P5[:, 256 + a:384 + a], us, 254.0, OP.is_lt, T.C37[:, 0:1], OP.mult, [("US", h), "C37"], [("W0", h)], 128, [5, 2 + h])
+        tt(T.OG[:], T.OF[:], T.P5[:, 0:256], OP.mult, ["OF", ("GG", 0), ("GG", 1)], ["OG"], 256, [5], 1.0)
+        tt(T.P5[:, 256:512], T.OF[:], T.P5[:, 256:512], OP.add, ["OF", ("W0", 0), ("W0", 1)], ["W1"], 256, [5], 1.0)
+        ts(T.GO[:], T.KD[:], 31.0, OP.is_equal, None, None, KDK, ["GO"], 16)
+        ts(T.NN[:], T.KD[:], 0.0, OP.is_lt, None, None, KDK, ["NN"], 16)
+        tt(T.GN[:], T.GO[:], T.NN[:], OP.add, ["GO", "NN"], ["GN"], 16)
+        ts(T.T36[:], T.GN[:], 36.0, OP.mult, 1.0, OP.add, ["GN"], ["T36"], 16)
+        tt(T.BM[:], T.T36[:], T.MF[:], OP.mult, ["T36", "MF"], ["BM"], 16)
+        ts(T.CA[:], T.GO[:], -1.0, OP.mult, 1.0, OP.add, ["GO"], ["CA"], 16)
+        tt(T.CB[:], T.CA[:], T.SX[:], OP.mult, ["CA", "SX"], ["CB"], 16)
+        UL = T.P6[:, 496:512]
+        tt(T.UM[:], T.GN[:], UL, OP.mult, ULK + ["GN"], ["UM"], 16, [6])
+        copy(T.UI[:], UL, ULK, ["UI"], 16, [6])
+        tt(T.MI[:], T.UM[:], T.BM[:], OP.add, ["UM", "BM"], ["MI"], 16)
+        ts(T.MI2[:], T.MI[:], 1023, OP.bitwise_and, None, None, ["MI"], ["MI2"], 16)
+        if t < 3:
+            copy(T.MS[:], T.MI2[:], ["MI2"], ["MS"], 16)
+            op("G", lambda q, n1=n1: send(q, T.MS, "MU%d" % n1, "m%%s%d" % n1), ["MS"], ["MU%ds" % n1], 0.5, (), ("ml%d" % n1, 8, 2.0))
+        else:
+            copy(T.YM[:], T.MI2[:], ["MI2"], ["YM"], 16)
+        tt(T.XA[:], T.MI2[:], T.GO[:], OP.mult, ["MI2", "GO"], ["XA"], 16)
+        tt(T.X[:], T.XA[:], T.CB[:], OP.add, ["XA", "CB"], ["X"], 16)
+        copy(T.XU[:], T.X[:], ["X"], ["XU"], 16)
+        ts(T.UI2[:], T.UI[:], 4095, OP.bitwise_and, None, None, ["UI"], ["UI2"], 16)
+        copy(T.UU[:], T.UI2[:], ["UI2"], ["UU"], 16)
+        tt(T.DM[:], T.SX[:], T.X[:], OP.subtract, ["SX", "X"], ["DM"], 16)
+        act(T.YB[:], T.BT[:].indirect(T.XU[:]), AF.Copy, ["BT", "XU"], ["YB"], 256, gather=True)
+        for gg in range(8):
+            if gg % 3 == 2: act(T.BD[:, :, gg, :], T.YB[:], AF.Copy, ["YB", "MSK"], [("BD", gg)], 256, scale=T.MSK[:, gg:gg + 1])
+            else: ts(T.BD[:, :, gg, :], T.YB[:], T.MSK[:, gg:gg + 1], OP.mult, None, None, ["YB", "MSK"], [("BD", gg)], 256, (), 0.5)
+        for cs, bank in (((14, 15), 1), ((12, 13), 4), ((10, 11), 0), ((7, 8, 9), 7), ((0, 1, 2, 3, 4, 5, 6), 6)):
+            off, P, lst, red = 0, T["P%d" % bank], [], []
+            for c in cs:
+                lh, nn = T.BD[:, c, :, :], 16 * c + 16
+                if c: lst.append((P[:, off:off + 16 * c], lh, T.YB[:, 0:16 * c], True, True))
+                lst.append((P[:, off + 16 * c:off + nn], lh, T.YB[:, 16 * c:nn], True, False))
+                lst.append((P[:, off + 16 * c:off + nn], T.IDN[:], T.TM[:], False, True))
+                red.append((c, off, nn))
+                off += nn
+            mm(lst, [("BD", gg) for gg in range(8)] + ["YB", "IDN", "TM"], [("E", bank)], off + 100 * len(cs), [bank])
+            for c, o, nn in red:
+                if c < 10: V(lambda q, c=c, o=o, nn=nn, P=P: q.tensor_reduce(T.DVX[:, c:c + 1], P[:, o:o + nn], AxisListType.X, OP.max), [("E", bank)], [("DF", c)], nn, [bank])
+                else: act(T.JK[:, 0:nn], P[:, o:o + nn], AF.Relu, [("E", bank)], ["JK", ("DF", c)], nn, [bank], bias=-15.0, accum_out=T.DA[:, c:c + 1])
+        ts(T.DF[:, 0:10], T.DVX[:, 0:10], 15.5, OP.is_ge, None, None, [("DF", c) for c in range(10)], ["DF0"], 10)
+        ts(T.DF[:, 10:16], T.DA[:, 10:16], 0.5, OP.is_ge, None, None, [("DF", c) for c in range(10, 16)], ["DF1"], 6)
+        tt(T.XD[:], T.DF[:], T.DM[:], OP.mult, ["DF0", "DF1", "DM"], ["XD"], 16)
+        tt(T.XF[:], T.XD[:], T.X[:], OP.add, ["XD", "X"], ["XF"], 16)
+        copy(T.XFU[:], T.XF[:], ["XF"], ["XFU"], 16)
+        V(lambda q: q.tensor_tensor(T.PP[:], T.IOTA[:].indirect(T.UU[:]), T.OG[:], OP.mult), ["IOTA", "UU", "OG"], ["PP"], 256, (), CG)
+        ts(T.SS[:], T.PP[:], 5, OP.arith_shift_right, None, None, ["PP"], ["SS"], 256)
+        tt(T.TT[:], T.SS[:], T.P5[:, 256:512], OP.add, ["SS", "W1"], ["TT"], 256, [5], 1.0)
+        ts(T.NW[:], T.TT[:], 4095, OP.bitwise_and, None, None, ["TT"], ["NW"], 256)
+        if t < 3:
+            copy(T.MC[:].indirect(T.XFU[:]), T.NW[:], ["NW", "XFU"], ["MC"], 256, (), 3.8)
+            ts(T.GOB[:], T.KD[:], 31.0, OP.is_equal, None, None, KDK, ["GOB"], 16)
+            mm([(T.P7[:, 496:512], T.ON[:, 0:128], T.GOB[:], True, True)], ["ON", "GOB"], ["APS"], 64, [7])
+            V(lambda q: q.tensor_reduce(T.AC[:], T.P7[:, 496:512], AxisListType.X, OP.add), ["APS"], ["AC"], 16, [7])
+            copy(T.AI[:], T.AC[:], ["AC"], ["AI"], 1)
+            ts(T.AP[:], T.AI[:], 1, OP.bitwise_and, None, None, ["AI"], ["AP"], 1)
+            ts(T.AT[:], T.AP[:], -128.0, OP.mult, -1472.0, OP.add, ["AP"], ["AT"], 1)
+            ts(T.TH[:], T.ON[:, 0:128], T.AT[:, 0:1], OP.mult, None, None, ["ON", "AT"], ["TH"], 128, (), 0.5)
+        else:
+            copy(T.MCF[:, 0:1024], T.MC[:, 0:1024], ["MC"], ["MCF"], 1024)
+            copy(T.MCF[:].indirect(T.XFU[:]), T.NW[:], ["NW", "XFU"], ["MCF"], 256, (), 3.8)
+            op("S", lambda q: q.dma_start(T.yz[:], T.ZF[:]), ["ZF0", "ZF1"], [], 0.1, (), ("so0", 16, 2))
+            op("S", lambda q: q.dma_start(T.ym[:], T.YM[:]), ["YM"], [], 0.1, (), ("so1", 16, 2))
+            op("S", lambda q: q.dma_start(T.ymc[:], T.MCF[:, 0:1024]), ["MCF"], [], 0.1, (), ("so2", 16, 4))
+    return ops
+
+
+def schedule(ops):
+    n = len(ops)
+    kids = [[] for _ in ops]
+    need = [0] * n
+    for i, o in enumerate(ops):
+        for d in o["hard"] | o["soft"]:
+            kids[d].append(i)
+            need[i] += 1
+    lat = [o["done"][2] if o["done"] else o["cost"] for o in ops]
+    prio = [0.0] * n
+    for i in range(n - 1, -1, -1):
+        prio[i] = lat[i] + 0.08 + max([prio[k] for k in kids[i]] + [0.0])
+    free, fin, start, est = {}, [0.0] * n, [0.0] * n, [0.0] * n
+    ready = [i for i in range(n) if need[i] == 0]
+    order = []
+    while ready:
+        beg = [max([est[i]] + ([min(free.get(e, 0.0) for e in ops[i]["eng"])] if ops[i]["eng"] else [])) for i in ready]
+        m = min(beg)
+        best = None
+        for i, b in zip(ready, beg):
+            if b <= m + EPS and (best is None or prio[i] > prio[best[0]]): best = (i, b)
+        i, b = best
+        o = ops[i]
+        ready.remove(i)
+        start[i], fin[i] = b, b + lat[i]
+        if o["eng"]:
+            e = min(o["eng"], key=lambda e: free.get(e, 0.0))
+            if len(o["eng"]) > 1: o["fn"] = (lambda f, e: lambda q: f(q, e))(o["fn"], e)
+            o["eng"] = e
+            free[e] = b + o["cost"]
+        order.append(i)
+        for k in kids[i]:
+            need[k] -= 1
+            w = 0.06 if ops[k]["eng"] == o["eng"] else WAKE
+            est[k] = max(est[k], fin[i] + w if i in ops[k]["hard"] else start[i])
+            if need[k] == 0: ready.append(k)
+    return order, start, fin
+
+
+def rank_program(g, core, T, topo):
+    rank = T.rank_of(core)
+    if rank is None:
+        return
+    nxt = T.cores[(rank + 1) % len(T.cores)]
+    ops = build(T, topo, core, nxt)
+    order, _, _ = schedule(ops)
+    Q = {"V": g.vector, "A": g.scalar, "T": g.tensor, "G": g, "S": g.sync}
+    cnt = {e: 0 for e in Q}
+    done, know = {}, {}
+    known = {e: {} for e in Q}
+    for i in order:
+        o = ops[i]
+        e = o["eng"]
+        if not e:
+            done[i] = o["done"][:2]
+            know[i] = {done[i][0]: done[i][1]}
+            continue
+        kn = known[e]
+        wants = {}
+        for d in o["hard"]:
+            s, v = done[d]
+            if kn.get(s, 0) < v and wants.get(s, (0, 0))[0] < v: wants[s] = (v, d)
+        for s in sorted(wants, key=lambda s: -wants[s][1]):
+            v, d = wants[s]
+            if kn.get(s, 0) >= v: continue
+            Q[e].wait_ge(T.sem[s], v)
+            for a, b in know[d].items():
+                if kn.get(a, 0) < b: kn[a] = b
+        x = o["fn"](Q[e])
+        if o["done"]:
+            done[i] = o["done"][:2]
+            if x is not None: x.then_inc(T.sem[done[i][0]], done[i][1])
+        else:
+            cnt[e] += 1
+            done[i] = ("s" + e, cnt[e])
+            x.then_inc(T.sem["s" + e], 1)
+        know[i] = dict(kn)
+        know[i][done[i][0]] = done[i][1]
+    kn = known["S"]
+    for i in reversed(order):
+        s, v = done[i]
+        if kn.get(s, 0) < v:
+            g.sync.wait_ge(T.sem[s], v)
+            kn[s] = v

@@ -5,9 +5,8 @@ SB = {
     "MC": (1280, I), "MCF": (1280, F), "PR": (4096, H), "AD": (4096, H), "GL": (1024, H), "M0": (16, I),
     "DV": (8, H), "WT": (1, H), "DH": (8, F), "DG": (1024, H), "OU": (256, U), "OF": (256, F), "Z": (256, H), "ZF": (256, F),
     "KV": (144, F), "BASE": (8, F), "IOTA": (4096, F), "BT": (1280, H), "BTI": (1280, I), "YB": (256, H),
-    "ON": (144, H), "IDN": (128, H), "NID": (128, H), "I128": (128, H), "BLK": (128, H), "BLB": (128, H), "CST": (128, H),
-    "RM": (2048, H), "RMN": (2048, H), "RMC": (2048, H), "RMW": (2048, H), "TH": (128, H), "MSK": (8, F),
-    "PI": (1, I), "PR16": (1, I), "R16": (1, F), "R32": (1, F), "C37": (1, F), "PW": (1, F), "TM": (16, H), "GOB": (16, H),
+    "ON": (256, H), "IDN": (128, H), "NID": (128, H), "I128": (128, H), "BLK": (128, H), "BLB": (128, H), "CST": (128, H), "CMB": (256, H),
+    "TH": (128, H), "MSK": (8, F), "PI": (1, I), "PR16": (1, I), "R16": (1, F), "R32": (1, F), "C37": (1, F), "PW": (1, F), "TM": (16, H), "GOB": (16, H),
     "MI": (16, I), "MI2": (16, I), "MS": (16, U), "XU": (16, U), "UI": (16, I), "UI2": (16, I), "UU": (16, U), "XFU": (16, U),
     "OG": (256, F), "PP": (256, I), "SS": (256, I), "TT": (256, I), "NW": (256, I), "JK": (256, H), "AC": (1, F), "AI": (1, I), "AP": (1, I), "AT": (1, F),
 }
@@ -19,15 +18,19 @@ for _h in "01":
 SCRATCH = {k: ("sbuf", [128, w], d) for k, (w, d) in SB.items()}
 for _h in "01":
     SCRATCH["C" + _h] = ("sbuf", [128, 8, 16, 18], H)
-    SCRATCH["BR" + _h] = ("sbuf", [128, 8, 18], H)
-SCRATCH["BD"] = ("sbuf", [128, 16, 8, 16], H)
+    for _x in "01": SCRATCH["BR" + _x + _h] = ("sbuf", [128, 8, 18], H)
+for _n in ("BD", "RM", "RMN", "RMC", "RMW"): SCRATCH[_n] = ("sbuf", [128, 16, 8, 16], H)
 for _b in range(8):
     SCRATCH["P%d" % _b] = ("psum", [128, 512], F)
-LOADS = {"m0": 2.2, "mc": 4.5, "gl": 6, "z0": 6.5, "pr": 9, "ad": 9, "dv": 3, "wt": 3}
+LOADS = {"m0": 2.2, "mc": 4.5, "gl": 6, "z0": 6.5, "pr": 7, "ad": 9, "dv": 3, "wt": 3}
 SEMAPHORES = ["sV", "sA", "sT", "sG", "so0", "so1", "so2"] + ["ld_" + n for n in LOADS] + ["%s%d" % (n, t) for n in ("zi", "mi", "zl", "ml") for t in range(1, 4)]
 
 CYC, WAKE, CG, PF = 0.00104, 0.12, 1.56, 0.5
-NA, EPS = 6, 0.1
+NAS = (0, 8)
+CHS = (4, 4)
+EPS, DV = 0.1, 0.0
+OFF = "GG=-2.8 KD1=-8.8 AB10=-8 MCF=9.2 BASE=-3.2 AP=3 TH=-0.7 C1=-2.8 VG1=-3.6 XD=-5.7 AI=3.2 X10=8.9 MS=-1.8 UI=0.5 BTI=-3.7 BR=-2 RMC=-14.8 JK=-17.1 BLK=1 SS=-19.5 RMN=-18.9 C37=-4.4 AB13=-10.9 SX=-3.6 MU0=-12.1 DG=1.1 OF=1.3 TM=-0.1 G1=4.2 US1=3.9 AB01=-0.8"
+PIN = "VG0=V AB12=A AB11=A PB02=A AB02=A PB13=V PB01=V PB00=V AB03=V AB10=A"
 
 
 def build(T, topo, core, nxt):
@@ -41,7 +44,7 @@ def build(T, topo, core, nxt):
         for k in writes:
             if k in wr: hard.add(wr[k])
             for r in rd.get(k, ()):
-                if r != i: (soft if ops[r]["eng"] == eng and eng in "VATGS" and ops[r]["done"] is None else hard).add(r)
+                if r != i: (soft if ops[r]["eng"] == eng and len(eng) == 1 and ops[r]["done"] is None else hard).add(r)
         for b in banks:
             for r in bk.setdefault(b, []):
                 if ops[r]["eng"] != eng: hard.add(r)
@@ -90,10 +93,9 @@ def build(T, topo, core, nxt):
     def load(q, name, dst, key):
         op(q, lambda e: e.dma_start(dst, T[name][:]), [], [key], 0.1, (), ("ld_" + name, 16, LOADS[name]))
 
-    load("S", "m0", T.M0[:], "M0"); load("S", "mc", T.MC[:, 0:1024], "MC"); load("S", "pr", T.PR[:], "PR"); load("S", "z0", T.ZI0[:], "ZI0")
-    load("A", "wt", T.WT[:], "WT"); load("A", "dv", T.DV[:], "DV"); load("A", "ad", T.AD[:], "AD"); load("A", "gl", T.GL[:], "GL")
-    fill(T.ON[:], 1.0, "ON", 144)
-    fill(T.RM[:], 1.0, "RM", 2048)
+    load("S", "m0", T.M0[:], "M0"); load("S", "mc", T.MC[:, 0:1024], "MC"); load("S", "pr", T.PR[:], "PR"); load("S", "ad", T.AD[:], "AD")
+    load("A", "wt", T.WT[:], "WT"); load("A", "dv", T.DV[:], "DV"); load("A", "z0", T.ZI0[:], "ZI0"); load("A", "gl", T.GL[:], "GL")
+    fill(T.ON[:], 1.0, "ON", 256)
     RM, imp = T.RM[:], {"allow_small_or_imprecise_dtypes": True}
     G(lambda q: q.iota(T.PI[:], [[0, 1]], 0, 1), [], ["PI"], 0.2)
     G(lambda q: q.iota(T.I16[:], [[1, 16]], 0, 0, **imp), [], ["I16"], 0.2)
@@ -102,20 +104,23 @@ def build(T, topo, core, nxt):
     G(lambda q: q.affine_select(T.BLK[:], T.BLB[:], [[16, 8], [0, 16]], OP.is_ge, 0.0, 15, -1), ["BLB"], ["BLK"], 0.5)
     G(lambda q: q.iota(T.KV[:], [[512, 8], [2, 18]], 14, 0, **imp), [], ["KV"], 0.5)
     G(lambda q: q.iota(T.SX[:], [[16, 16]], 1024, 0, **imp), [], ["SX"], 0.2)
-    G(lambda q: q.affine_select(RM, RM, [[-1, 16], [0, 8], [1, 16]], OP.is_equal, 0.0, 0, 0), ["RM"], ["RM"], 4.0)
-    G(lambda q: q.affine_select(RM, RM, [[0, 16], [-16, 8], [0, 16]], OP.is_ge, 0.0, 0, 1), ["RM"], ["RM"], 4.0)
-    G(lambda q: q.affine_select(RM, RM, [[0, 16], [16, 8], [0, 16]], OP.is_ge, 0.0, 15, -1), ["RM"], ["RM"], 4.0)
-    G(lambda q: q.iota(T.IOTA[:], [[1, 4096]], 0, 0, **imp), [], ["IOTA"], 8.0)
+    G(lambda q: q.affine_select(T.CMB[:], T.ON[:], [[-1, 16], [1, 16]], OP.is_equal, 0.0, 0, 0), ["ON"], ["CMB"], 0.5)
+    G(lambda q: q.iota(T.IOTA[:], [[1, 4096]], 0, 0, **imp), ["BLK", "CMB", "IDN", "KV", "SX", "I16", "PI"], ["IOTA"], 8.0)
+    copy(T.MSK[:], T.BLK[:, 0:128:16], ["BLK"], ["MSK"], 8)
+    for x in range(8): ts(T.RM[:, :, x, :], T.CMB[:], T.MSK[:, x:x + 1], OP.mult, None, None, ["MSK", "CMB"], [("RM", x)], 256, (), 0.5)
+    RMK = [("RM", x) for x in range(8)]
     for h in range(2):
         AB, PB = T["AB%d" % h], T["PB%d" % h]
-        fill(AB[:, 15:4112:2], 0.0, "ABo%d" % h, 2049)
-        fill(AB[:, 15:4112:32], -256.0, "ABo%d" % h, 129)
-        fill(PB[:, 18:4112:2], 0.0, "PBz%d" % h, 2047)
+        if h: act(AB[:, 15:4112:2], T.AB0[:, 15:4112:2], AF.Copy, ["ABo0"], ["ABo1"], 2049)
+        else:
+            fill(AB[:, 15:4112:2], 0.0, "ABo0", 2049)
+            fill(AB[:, 15:4112:32], -256.0, "ABo0", 129)
+        act(PB[:, 18:4112:2], T.AB0[:, 15:4108:2], AF.Copy, ["ABo0"], ["PBz%d" % h], 2047, scale=0.0)
         fill(T["C%d" % h][:, :, :, 0], 1.0, ("C", h, 0), 128)
-    fill(T.BR0[:, :, 0:18 - NA], 1.0, ("BR", 0), 144)
-    fill(T.BR0[:, :, 18 - NA:18], 2.0, ("BR", 1), 144)
-    fill(T.BR1[:, :, 0:18 - NA], 0.0, ("BR", 2), 144)
-    fill(T.BR1[:, :, 18 - NA:18], 1.0, ("BR", 3), 144)
+    for h in range(2):
+        for x in range(2):
+            if NAS[h]: fill(T["BR%d%d" % (x, h)][:, :, 18 - NAS[h]:18], 2.0 - x, ("BR", h), 144)
+            fill(T["BR%d%d" % (x, h)][:, :, 0:18 - NAS[h]], 1.0 - x, ("BR", h), 144)
     fill(T.CST[:], 2048.0, "CST", 128)
     fill(T.TH[:], -1472.0, "TH", 128)
     ts(T.PR16[:], T.PI[:], 15, OP.bitwise_and, None, None, ["PI"], ["PR16"], 1)
@@ -137,10 +142,9 @@ def build(T, topo, core, nxt):
     ts(T.BT[:], T.BTI[:], 2.0, OP.mult, -1.0, OP.add, ["BTI"], ["BT"], 1280)
     ts(T.NID[:], T.IDN[:], -1.0, OP.mult, None, None, ["IDN"], ["NID"], 128, (), 0.5)
     ts(T.I128[:], T.IDN[:], 128.0, OP.mult, None, None, ["IDN"], ["I128"], 128, (), 0.5)
-    act(T.RMC[:], RM, AF.Copy, ["RM"], ["RMC"], 2048, scale=16384.0)
-    act(T.RMN[:], RM, AF.Copy, ["RM"], ["RMN"], 2048, scale=-1.0)
-    ts(T.RMW[:], RM, T.WT[:, 0:1], OP.mult, None, None, ["RM", "WT"], ["RMW"], 2048, (), 0.5)
-    copy(T.MSK[:], T.BLK[:, 0:128:16], ["BLK"], ["MSK"], 8)
+    act(T.RMC[:], RM, AF.Copy, RMK, ["RMC"], 2048, scale=16384.0)
+    act(T.RMN[:], RM, AF.Copy, RMK, ["RMN"], 2048, scale=-1.0)
+    ts(T.RMW[:], RM, T.WT[:, 0:1], OP.mult, None, None, RMK + ["WT"], ["RMW"], 2048, (), 0.5)
     ts(T.DH[:], T.DV[:], -0.5, OP.mult, None, None, ["DV"], ["DH"], 8)
     for j in range(8):
         ts(T.DG[:, 128 * j:128 * j + 128], T.IDN[:], T.DH[:, j:j + 1], OP.mult, None, None, ["IDN", "DH"], [("DG", j)], 128, (), 0.5)
@@ -150,7 +154,7 @@ def build(T, topo, core, nxt):
         ZI, MU = T["ZI%d" % t], T["MU%d" % t]
         zk, mk = "ZI%d" % t, "MU%d" % t
         if t:
-            nw = 8
+            nw = len(topo.engines(core, nxt))
             op("", None, [zk + "s"], [zk], 0, (), ("zi%d" % t, nw, 3.0))
             op("", None, [mk + "s"], [mk], 0, (), ("mi%d" % t, nw, 3.0))
         for h in range(2):
@@ -159,12 +163,11 @@ def build(T, topo, core, nxt):
             act(T["G%d" % h][:], T.GL[:].indirect(MU[:, 8 * h:8 * h + 8]), AF.Copy, ["GL", mk], ["G%d" % h], 128, gather=True)
         copy(T.MF[:], MU[:], [mk], ["MF"], 16)
         for h in range(2):
-            Zb, Xb, Eb, Fb = T["P%d" % h], T["P%d" % (2 + h)], T["P%d" % (6 + h)], T["P%d" % (5 - h)]
+            Zb, Xb, Eb = T["P%d" % h], T["P%d" % (2 + h)], T["P%d" % (6 + h)]
             AB, PB, KB, C = T["AB%d" % h], T["PB%d" % h], T["KB%d" % h], T["C%d" % h]
             KS, KU, vg, sg, T2, R0, G_ = [T[n + str(h)] for n in ("KS", "KU", "VG", "SG", "T2", "R0", "G")]
-            a, b = 128 * h, 128 * h + 128
+            a, b, ch, NA = 128 * h, 128 * h + 128, CHS[h], NAS[h]
             mm([(Zb[:, 0:128], T.IDN[:], ZI[:, a:b], True, True)], [zk, "IDN"], ["ZP%d" % h], 128, [h])
-            ch = 4
             n = 128 // ch
             for c in range(ch):
                 lo, s0 = 32 * n * c, a + n * c
@@ -178,15 +181,17 @@ def build(T, topo, core, nxt):
             mm([(Eb[:, 0:128], T.IDN[:], KB[:, 1:4096:32], True, False), (Eb[:, 0:128], T.IDN[:], AB[:, 16:4112:32], False, True)],
                ["IDN", "KB%d" % h] + ak, ["E0%d" % h], 256, [6 + h])
             act(R0[:], Eb[:, 0:128], AF.Relu, ["E0%d" % h], ["R0%d" % h], 128, [6 + h])
-            us, lst = Xb[:, 272:400], []
+            us = T["P%d" % (4 + h)][:, 384 * h:384 * h + 128]
             for k in range(16):
-                lst.append((us, T.RM[:, 128 * k:128 * k + 128], KB[:, 2 * k + 1:4096:32], k == 0, False))
-                lst.append((us, T.RMN[:, 128 * k:128 * k + 128], KB[:, 2 * k:4096:32] if k else R0[:], False, k == 15))
-            mm(lst, ["RM", "RMN", "KB%d" % h, "R0%d" % h], [("US", h)], 32 * 128, [2 + h])
+                if k % 4 == 0: lst = []
+                lst.append((us, T.RM[:, k, :, :], KB[:, 2 * k + 1:4096:32], k == 0, False))
+                lst.append((us, T.RMN[:, k, :, :], KB[:, 2 * k:4096:32] if k else R0[:], False, k == 15))
+                if k % 4 == 3: mm(lst, RMK + ["RMN", "KB%d" % h, "R0%d" % h, ("UO", h, k)], [("US", h, k), ("UO", h, k - 4)], 8 * 128, [4 + h])
             zsrc, zkey = ZI[:, a:b], zk
             kpos = [2 * k - 1 if k else 0 for k in range(17)]
             for j in range(2):
-                for B, bank, ks in ((Eb, 6 + h, range(17 - NA, 17 - NA // 2)), (Fb, 5 - h, range(17 - NA // 2, 17))):
+                for B, bank, ks in ((T.P7, 7, range(17 - NA, 17 - NA + min(4, NA))), (T.P6, 6, range(17 - NA + min(4, NA), 17))):
+                    if not ks: continue
                     lst = []
                     for i, k in enumerate(ks):
                         lst.append((B[:, 128 * i:128 * i + 128], T.IDN[:], zsrc, True, False))
@@ -197,9 +202,9 @@ def build(T, topo, core, nxt):
                 for k in range(17 - NA):
                     tt(C[:, :, :, k + 1], KB[:, kpos[k]:4096:32], Zb[:, 0:128], OP.is_le, ["KB%d" % h, "ZP%d" % h], [("C", h, k + 1)], 128, [h], 1.0)
                 cp = Xb[:, 0:144]
-                lst = [(cp, T.TH[:], T.BR0[:], True, False), (cp, T.CST[:], T.BR1[:], False, False)]
-                lst += [(cp, T.RMC[:, 128 * r:128 * r + 128], C[:, :, r, :], False, r == 15) for r in range(16)]
-                mm(lst, [("C", h, k) for k in range(18)] + [("BR", x) for x in range(4)] + ["RMC", "CST", "TH"], ["CP%d" % h], 18 * 144, [2 + h])
+                lst = [(cp, T.TH[:], T["BR0%d" % h][:], True, False)] + ([(cp, T.CST[:], T["BR1%d" % h][:], False, False)] if NA else [])
+                lst += [(cp, T.RMC[:, r, :, :], C[:, :, r, :], False, r == 15) for r in range(16)]
+                mm(lst, [("C", h, k) for k in range(18)] + [("BR", h)] + ["RMC", "CST", "TH"], ["CP%d" % h], 18 * 144, [2 + h])
                 V(lambda q, KS=KS, cp=cp: q.tensor_tensor_scan(KS[:], cp, T.KV[:], 0.0, OP.max, OP.min), ["CP%d" % h, "KV"], ["KS%d" % h], 144, [2 + h])
                 copy(KU[:], KS[:, 17:144:18], ["KS%d" % h], ["KU%d" % h], 8)
                 abk = ak + ["ABo%d" % h, "KU%d" % h]
@@ -216,24 +221,24 @@ def build(T, topo, core, nxt):
                 act(T.Z[:, a:b], xs, AF.Abs, xr, ["Z%d" % h], 128, [2 + h], bias=bias)
                 if t == 3 and j == 1: act(T.ZF[:, a:b], xs, AF.Abs, xr, ["ZF%d" % h], 128, [2 + h], bias=bias)
                 zsrc, zkey = T.Z[:, a:b], "Z%d" % h
-            ul = T.P6[:, 496 + 8 * h:504 + 8 * h]
-            mm([(ul, T.RMW[:, 128 * r:128 * r + 128], T.Z[:, a + r:b:16], r == 0, r == 15) for r in range(16)], ["RMW", "Z%d" % h], [("UL", h)], 1024, [6])
+            ul = T.P2[:, 400 + 8 * h:408 + 8 * h]
+            mm([(ul, T.RMW[:, r, :, :], T.Z[:, a + r:b:16], r == 0, r == 15) for r in range(16)], ["RMW", "Z%d" % h], [("UL", h)], 1024, [2])
             tt(T.KD[:, 8 * h:8 * h + 8], KS[:, 17:144:18], T.BASE[:], OP.subtract, ["KS%d" % h, "BASE"], [("KD", h)], 8)
 
         def send(q, src, name, sem):
             rid, pid, _ = topo.addr(nxt)
             q.remote_dma(T[name][:], src[:], T.sem[sem % "i"], T.sem[sem % "l"], pid, rid, topo.mask(core, nxt))
-        n1 = t + 1
+        n1, ne = t + 1, len(topo.engines(core, nxt))
         if t < 3:
-            op("G", lambda q, n1=n1: send(q, T.Z, "ZI%d" % n1, "z%%s%d" % n1), ["Z0", "Z1"], ["ZI%ds" % n1], 0.5, (), ("zl%d" % n1, 8, 2.0))
+            op("G", lambda q, n1=n1: send(q, T.Z, "ZI%d" % n1, "z%%s%d" % n1), ["Z0", "Z1"], ["ZI%ds" % n1], 0.5, (), ("zl%d" % n1, ne, 2.0))
         KDK, ULK = [("KD", 0), ("KD", 1)], [("UL", 0), ("UL", 1)]
         copy(T.OF[:], T.OU[:], [("OU", 0), ("OU", 1)], ["OF"], 256)
         for h in range(2):
-            us, a = T["P%d" % (2 + h)][:, 272:400], 128 * h
-            ts(T.P5[:, a:a + 128], us, 254.0, OP.is_lt, None, None, [("US", h)], [("GG", h)], 128, [5, 2 + h])
-            ts(T.P5[:, 256 + a:384 + a], us, 254.0, OP.is_lt, T.C37[:, 0:1], OP.mult, [("US", h), "C37"], [("W0", h)], 128, [5, 2 + h])
-        tt(T.OG[:], T.OF[:], T.P5[:, 0:256], OP.mult, ["OF", ("GG", 0), ("GG", 1)], ["OG"], 256, [5], 1.0)
-        tt(T.P5[:, 256:512], T.OF[:], T.P5[:, 256:512], OP.add, ["OF", ("W0", 0), ("W0", 1)], ["W1"], 256, [5], 1.0)
+            us, a, uk = T["P%d" % (4 + h)][:, 384 * h:384 * h + 128], 128 * h, [("US", h, k) for k in (3, 7, 11, 15)]
+            ts(T.P4[:, 128 + a:256 + a], us, 254.0, OP.is_lt, None, None, uk, [("GG", h)], 128, [4, 5])
+            ts(T.P5[:, a:a + 128], us, 254.0, OP.is_lt, T.C37[:, 0:1], OP.mult, uk + ["C37"], [("W0", h)], 128, [4, 5])
+        tt(T.OG[:], T.OF[:], T.P4[:, 128:384], OP.mult, ["OF", ("GG", 0), ("GG", 1)], ["OG"], 256, [4], 1.0)
+        tt(T.P5[:, 0:256], T.OF[:], T.P5[:, 0:256], OP.add, ["OF", ("W0", 0), ("W0", 1)], ["W1"], 256, [5], 1.0)
         ts(T.GO[:], T.KD[:], 31.0, OP.is_equal, None, None, KDK, ["GO"], 16)
         ts(T.NN[:], T.KD[:], 0.0, OP.is_lt, None, None, KDK, ["NN"], 16)
         tt(T.GN[:], T.GO[:], T.NN[:], OP.add, ["GO", "NN"], ["GN"], 16)
@@ -241,14 +246,14 @@ def build(T, topo, core, nxt):
         tt(T.BM[:], T.T36[:], T.MF[:], OP.mult, ["T36", "MF"], ["BM"], 16)
         ts(T.CA[:], T.GO[:], -1.0, OP.mult, 1.0, OP.add, ["GO"], ["CA"], 16)
         tt(T.CB[:], T.CA[:], T.SX[:], OP.mult, ["CA", "SX"], ["CB"], 16)
-        UL = T.P6[:, 496:512]
-        tt(T.UM[:], T.GN[:], UL, OP.mult, ULK + ["GN"], ["UM"], 16, [6])
-        copy(T.UI[:], UL, ULK, ["UI"], 16, [6])
+        UL = T.P2[:, 400:416]
+        tt(T.UM[:], T.GN[:], UL, OP.mult, ULK + ["GN"], ["UM"], 16, [2])
+        copy(T.UI[:], UL, ULK, ["UI"], 16, [2])
         tt(T.MI[:], T.UM[:], T.BM[:], OP.add, ["UM", "BM"], ["MI"], 16)
         ts(T.MI2[:], T.MI[:], 1023, OP.bitwise_and, None, None, ["MI"], ["MI2"], 16)
         if t < 3:
             copy(T.MS[:], T.MI2[:], ["MI2"], ["MS"], 16)
-            op("G", lambda q, n1=n1: send(q, T.MS, "MU%d" % n1, "m%%s%d" % n1), ["MS"], ["MU%ds" % n1], 0.5, (), ("ml%d" % n1, 8, 2.0))
+            op("G", lambda q, n1=n1: send(q, T.MS, "MU%d" % n1, "m%%s%d" % n1), ["MS"], ["MU%ds" % n1], 0.5, (), ("ml%d" % n1, ne, 2.0))
         else:
             copy(T.YM[:], T.MI2[:], ["MI2"], ["YM"], 16)
         tt(T.XA[:], T.MI2[:], T.GO[:], OP.mult, ["MI2", "GO"], ["XA"], 16)
@@ -259,9 +264,9 @@ def build(T, topo, core, nxt):
         tt(T.DM[:], T.SX[:], T.X[:], OP.subtract, ["SX", "X"], ["DM"], 16)
         act(T.YB[:], T.BT[:].indirect(T.XU[:]), AF.Copy, ["BT", "XU"], ["YB"], 256, gather=True)
         for gg in range(8):
-            if gg % 3 == 2: act(T.BD[:, :, gg, :], T.YB[:], AF.Copy, ["YB", "MSK"], [("BD", gg)], 256, scale=T.MSK[:, gg:gg + 1])
+            if gg in (1, 4, 7): act(T.BD[:, :, gg, :], T.YB[:], AF.Copy, ["YB", "MSK"], [("BD", gg)], 256, scale=T.MSK[:, gg:gg + 1])
             else: ts(T.BD[:, :, gg, :], T.YB[:], T.MSK[:, gg:gg + 1], OP.mult, None, None, ["YB", "MSK"], [("BD", gg)], 256, (), 0.5)
-        for cs, bank in (((14, 15), 1), ((12, 13), 4), ((10, 11), 0), ((7, 8, 9), 7), ((0, 1, 2, 3, 4, 5, 6), 6)):
+        for cs, bank in (((14, 15), 1), ((12, 13), 3), ((10, 11), 0), ((7, 8, 9), 7), ((0, 1, 2, 3, 4, 5, 6), 6)):
             off, P, lst, red = 0, T["P%d" % bank], [], []
             for c in cs:
                 lh, nn = T.BD[:, c, :, :], 16 * c + 16
@@ -281,7 +286,7 @@ def build(T, topo, core, nxt):
         copy(T.XFU[:], T.XF[:], ["XF"], ["XFU"], 16)
         V(lambda q: q.tensor_tensor(T.PP[:], T.IOTA[:].indirect(T.UU[:]), T.OG[:], OP.mult), ["IOTA", "UU", "OG"], ["PP"], 256, (), CG)
         ts(T.SS[:], T.PP[:], 5, OP.arith_shift_right, None, None, ["PP"], ["SS"], 256)
-        tt(T.TT[:], T.SS[:], T.P5[:, 256:512], OP.add, ["SS", "W1"], ["TT"], 256, [5], 1.0)
+        tt(T.TT[:], T.SS[:], T.P5[:, 0:256], OP.add, ["SS", "W1"], ["TT"], 256, [5], 1.0)
         ts(T.NW[:], T.TT[:], 4095, OP.bitwise_and, None, None, ["TT"], ["NW"], 256)
         if t < 3:
             copy(T.MC[:].indirect(T.XFU[:]), T.NW[:], ["NW", "XFU"], ["MC"], 256, (), 3.8)
@@ -301,7 +306,16 @@ def build(T, topo, core, nxt):
     return ops
 
 
+def name_of(o):
+    w = o["w"][0] if o["w"] else "out"
+    if not isinstance(w, tuple): return w
+    piece = w[0] in ("PB", "AB")
+    return w[0] + (str(w[1]) if piece or w[0] in ("C", "OU", "US", "UL", "KD", "D") else "") + (str(w[2]) if piece else "")
+
+
 def schedule(ops):
+    off = {k: float(v) for k, v in (x.split("=") for x in OFF.split())}
+    pin = dict(x.split("=") for x in PIN.split())
     n = len(ops)
     kids = [[] for _ in ops]
     need = [0] * n
@@ -313,28 +327,37 @@ def schedule(ops):
     prio = [0.0] * n
     for i in range(n - 1, -1, -1):
         prio[i] = lat[i] + 0.08 + max([prio[k] for k in kids[i]] + [0.0])
-    free, fin, start, est = {}, [0.0] * n, [0.0] * n, [0.0] * n
+    prio = [p + off.get(name_of(o), 0.0) for p, o in zip(prio, ops)]
+    for o in ops:
+        if len(o["eng"]) > 1: o["cand"] = pin.get(name_of(o), o["eng"])
+        else: o["cand"] = o["eng"]
+    free, fin, start, est = dict.fromkeys("VATGS", 0.0), [0.0] * n, [0.0] * n, [0.0] * n
     ready = [i for i in range(n) if need[i] == 0]
     order = []
     while ready:
-        beg = [max([est[i]] + ([min(free.get(e, 0.0) for e in ops[i]["eng"])] if ops[i]["eng"] else [])) for i in ready]
-        m = min(beg)
+        beg = []
+        for i in ready:
+            e = ops[i]["cand"]
+            beg.append(est[i] if not e else max(est[i], free[e]) if len(e) == 1 else max(est[i], min(free["V"] + DV, free["A"])))
+        m = min(beg) + EPS
         best = None
         for i, b in zip(ready, beg):
-            if b <= m + EPS and (best is None or prio[i] > prio[best[0]]): best = (i, b)
+            if b <= m and (best is None or prio[i] > prio[best[0]]): best = (i, b)
         i, b = best
         o = ops[i]
         ready.remove(i)
-        start[i], fin[i] = b, b + lat[i]
-        if o["eng"]:
-            e = min(o["eng"], key=lambda e: free.get(e, 0.0))
-            if len(o["eng"]) > 1: o["fn"] = (lambda f, e: lambda q: f(q, e))(o["fn"], e)
-            o["eng"] = e
+        e = o["cand"]
+        if len(e) > 1: e = "V" if free["V"] + DV <= free["A"] else "A"
+        if len(o["eng"]) > 1: o["fn"] = (lambda f, e: lambda q: f(q, e))(o["fn"], e)
+        o["eng"] = o["cand"] = e
+        if e:
+            b = max(est[i], free[e])
             free[e] = b + o["cost"]
+        start[i], fin[i] = b, b + lat[i]
         order.append(i)
         for k in kids[i]:
             need[k] -= 1
-            w = 0.06 if ops[k]["eng"] == o["eng"] else WAKE
+            w = 0.06 if ops[k]["cand"] == e else WAKE
             est[k] = max(est[k], fin[i] + w if i in ops[k]["hard"] else start[i])
             if need[k] == 0: ready.append(k)
     return order, start, fin

from concourse.mybir import dt, AluOpType as OP, AxisListType, ActivationFunctionType as AF

F, H, I, U = "float32", "bfloat16", "int32", "uint16"
SB = {
    "MC": (1280, I), "MCF": (1280, F), "PR": (4096, H), "AD": (4096, H), "GL": (1024, H), "M0": (16, I),
    "DV": (8, H), "WT": (1, H), "DH": (8, F), "DG": (1024, H), "OU": (256, U), "OF": (256, F), "Z": (256, H), "ZF": (256, F),
    "KV": (144, F), "BASE": (8, F), "IOTA": (4096, F), "BT": (1280, H), "BTI": (1280, I), "YB": (256, H),
    "ON": (256, H), "IDN": (128, H), "NID": (128, H), "I128": (128, H), "BLK": (128, H), "BLB": (128, H), "CST": (128, H), "CMB": (256, H),
    "TH": (128, H), "MSK": (8, F), "PI": (1, I), "PR16": (1, I), "R16": (1, F), "R32": (1, F), "C37": (1, F), "PW": (1, F), "TM": (16, H), "GOB": (16, H),
    "MI": (16, I), "MI2": (16, I), "MS": (16, U), "XU": (16, U), "UI": (16, I), "UI2": (16, I), "UU": (16, U), "XFU": (16, U),
    "OG": (256, F), "PP": (256, I), "SS": (256, I), "TT": (256, I), "NW": (256, I), "JK": (256, H), "AC": (1, F), "AI": (1, I), "AP": (1, I), "AT": (1, F),
}
for _n in "I16 E16 PWR SX KD GO NN GN T36 BM MF CA CB UM YM XA X DM DVX DA DF XD XF".split(): SB[_n] = (16, F)
for _h in "0123": SB["ZI" + _h], SB["MU" + _h] = (256, H), (16, U)
for _h in "01":
    for _n, _w, _d in (("G", 128, H), ("AB", 4112, H), ("PB", 4112, H), ("KB", 4096, H), ("KS", 144, F), ("KU", 8, U), ("VG", 128, H), ("SG", 128, H), ("T2", 128, H), ("R0", 128, H)):
        SB[_n + _h] = (_w, _d)
SCRATCH = {k: ("sbuf", [128, w], d) for k, (w, d) in SB.items()}
for _h in "01":
    SCRATCH["C" + _h] = ("sbuf", [128, 8, 16, 18], H)
    for _x in "01": SCRATCH["BR" + _x + _h] = ("sbuf", [128, 8, 18], H)
for _n in ("BD", "RM", "RMN", "RMC", "RMW"): SCRATCH[_n] = ("sbuf", [128, 16, 8, 16], H)
for _b in range(8):
    SCRATCH["P%d" % _b] = ("psum", [128, 512], F)
LOADS = {"m0": 2.2, "mc": 4.5, "gl": 6, "z0": 6.5, "pr": 7, "ad": 9, "dv": 3, "wt": 3}
SEMAPHORES = ["sV", "sA", "sT", "sG", "so0", "so1", "so2"] + ["ld_" + n for n in LOADS] + ["%s%d" % (n, t) for n in ("zi", "mi", "zl", "ml") for t in range(1, 4)]

CYC, WAKE, CG, PF = 0.00104, 0.12, 1.56, 0.5
NAS = (0, 8)
CHS = (4, 4)
EPS, DV = 0.1, 0.0
OFF = "GG=-2.8 KD1=-8.8 AB10=-8 MCF=9.2 BASE=-3.2 AP=3 TH=-0.7 C1=-2.8 VG1=-3.6 XD=-5.7 AI=3.2 X10=8.9 MS=-1.8 UI=0.5 BTI=-3.7 BR=-2 RMC=-14.8 JK=-17.1 BLK=1 SS=-19.5 RMN=-18.9 C37=-4.4 AB13=-10.9 SX=-3.6 MU0=-12.1 DG=1.1 OF=1.3 TM=-0.1 G1=4.2 US1=3.9 AB01=-0.8"
PIN = "VG0=V AB12=A AB11=A PB02=A AB02=A PB13=V PB01=V PB00=V AB03=V AB10=A"


def build(T, topo, core, nxt):
    ops, wr, rd, bk = [], {}, {}, {}

    def op(eng, fn, reads, writes, cost, banks=(), done=None):
        i = len(ops)
        hard, soft = set(), set()
        for k in reads:
            if k in wr: hard.add(wr[k])
        for k in writes:
            if k in wr: hard.add(wr[k])
            for r in rd.get(k, ()):
                if r != i: (soft if ops[r]["eng"] == eng and len(eng) == 1 and ops[r]["done"] is None else hard).add(r)
        for b in banks:
            for r in bk.setdefault(b, []):
                if ops[r]["eng"] != eng: hard.add(r)
            bk[b].append(i)
        for k in reads: rd.setdefault(k, []).append(i)
        for k in writes:
            wr[k] = i
            rd[k] = []
        ops.append({"eng": eng, "fn": fn, "hard": hard, "soft": soft - hard, "cost": cost, "done": done, "w": writes})

    def V(fn, reads, writes, n, banks=(), f=1.0):
        op("V", fn, reads, writes, max(64, n * f) * CYC + 0.02, banks)

    def G(fn, reads, writes, cost):
        op("G", fn, reads, writes, cost)

    def copy(o, i, r, w, n, banks=(), f=1.0):
        V(lambda q: q.tensor_copy(o, i), r, w, n, banks, f)

    def ts(o, i, s1, o1, s2, o2, r, w, n, banks=(), f=1.0):
        if o2 is None: V(lambda q: q.tensor_scalar(o, i, s1, None, o1), r, w, n, banks, f)
        else: V(lambda q: q.tensor_scalar(o, i, s1, s2, o1, o2), r, w, n, banks, f)

    def tt(o, a, b, f, r, w, n, banks=(), c=2.0):
        V(lambda q: q.tensor_tensor(o, a, b, f), r, w, n, banks, c)

    def act(o, i, func, r, w, n, banks=(), gather=False, **kw):
        op("A", lambda q: q.activation(o, i, func, **kw), r, w, 0.08 + n * CG * CYC if gather else max(64, n) * CYC + 0.05, banks)

    def gath(o, i, neg, r, w, n):
        def fn(q, e):
            if e == "A": return q.activation(o, i, AF.Copy, scale=-1.0 if neg else 1.0)
            return q.tensor_scalar(o, i, -1.0, None, OP.mult) if neg else q.tensor_copy(o, i)
        op("VA", fn, r, w, 0.08 + n * CG * CYC)

    def fill(o, c, w, n):
        V(lambda q: q.memset(o, c), [], [w], n, (), 0.5)

    def mm(lst, r, w, n, banks):
        def fn(q):
            x = None
            for (o, l, rr, s, e) in lst: x = q.matmul(o, l, rr, s, e)
            return x
        op("T", fn, r, w, n * CYC * PF + 0.05, banks)

    def load(q, name, dst, key):
        op(q, lambda e: e.dma_start(dst, T[name][:]), [], [key], 0.1, (), ("ld_" + name, 16, LOADS[name]))

    load("S", "m0", T.M0[:], "M0"); load("S", "mc", T.MC[:, 0:1024], "MC"); load("S", "pr", T.PR[:], "PR"); load("S", "ad", T.AD[:], "AD")
    load("A", "wt", T.WT[:], "WT"); load("A", "dv", T.DV[:], "DV"); load("A", "z0", T.ZI0[:], "ZI0"); load("A", "gl", T.GL[:], "GL")
    fill(T.ON[:], 1.0, "ON", 256)
    RM, imp = T.RM[:], {"allow_small_or_imprecise_dtypes": True}
    G(lambda q: q.iota(T.PI[:], [[0, 1]], 0, 1), [], ["PI"], 0.2)
    G(lambda q: q.iota(T.I16[:], [[1, 16]], 0, 0, **imp), [], ["I16"], 0.2)
    G(lambda q: q.affine_select(T.IDN[:], T.ON[:, 0:128], [[-1, 128]], OP.is_equal, 0.0, 0, 1), ["ON"], ["IDN"], 0.5)
    G(lambda q: q.affine_select(T.BLB[:], T.ON[:, 0:128], [[-16, 8], [0, 16]], OP.is_ge, 0.0, 0, 1), ["ON"], ["BLB"], 0.5)
    G(lambda q: q.affine_select(T.BLK[:], T.BLB[:], [[16, 8], [0, 16]], OP.is_ge, 0.0, 15, -1), ["BLB"], ["BLK"], 0.5)
    G(lambda q: q.iota(T.KV[:], [[512, 8], [2, 18]], 14, 0, **imp), [], ["KV"], 0.5)
    G(lambda q: q.iota(T.SX[:], [[16, 16]], 1024, 0, **imp), [], ["SX"], 0.2)
    G(lambda q: q.affine_select(T.CMB[:], T.ON[:], [[-1, 16], [1, 16]], OP.is_equal, 0.0, 0, 0), ["ON"], ["CMB"], 0.5)
    G(lambda q: q.iota(T.IOTA[:], [[1, 4096]], 0, 0, **imp), ["BLK", "CMB", "IDN", "KV", "SX", "I16", "PI"], ["IOTA"], 8.0)
    copy(T.MSK[:], T.BLK[:, 0:128:16], ["BLK"], ["MSK"], 8)
    for x in range(8): ts(T.RM[:, :, x, :], T.CMB[:], T.MSK[:, x:x + 1], OP.mult, None, None, ["MSK", "CMB"], [("RM", x)], 256, (), 0.5)
    RMK = [("RM", x) for x in range(8)]
    for h in range(2):
        AB, PB = T["AB%d" % h], T["PB%d" % h]
        if h: act(AB[:, 15:4112:2], T.AB0[:, 15:4112:2], AF.Copy, ["ABo0"], ["ABo1"], 2049)
        else:
            fill(AB[:, 15:4112:2], 0.0, "ABo0", 2049)
            fill(AB[:, 15:4112:32], -256.0, "ABo0", 129)
        act(PB[:, 18:4112:2], T.AB0[:, 15:4108:2], AF.Copy, ["ABo0"], ["PBz%d" % h], 2047, scale=0.0)
        fill(T["C%d" % h][:, :, :, 0], 1.0, ("C", h, 0), 128)
    for h in range(2):
        for x in range(2):
            if NAS[h]: fill(T["BR%d%d" % (x, h)][:, :, 18 - NAS[h]:18], 2.0 - x, ("BR", h), 144)
            fill(T["BR%d%d" % (x, h)][:, :, 0:18 - NAS[h]], 1.0 - x, ("BR", h), 144)
    fill(T.CST[:], 2048.0, "CST", 128)
    fill(T.TH[:], -1472.0, "TH", 128)
    ts(T.PR16[:], T.PI[:], 15, OP.bitwise_and, None, None, ["PI"], ["PR16"], 1)
    copy(T.R16[:], T.PR16[:], ["PR16"], ["R16"], 1)
    ts(T.R32[:], T.R16[:], 32.0, OP.mult, None, None, ["R16"], ["R32"], 1)
    ts(T.C37[:], T.R16[:], 37.0, OP.mult, None, None, ["R16"], ["C37"], 1)
    ts(T.KV[:], T.KV[:], T.R32[:, 0:1], OP.add, None, None, ["R32", "KV"], ["KV"], 144)
    ts(T.KV[:, 0:144:18], T.KV[:, 0:144:18], 1.0, OP.add, None, None, ["KV"], ["KV"], 8)
    ts(T.KV[:, 17:144:18], T.KV[:, 17:144:18], -1.0, OP.add, None, None, ["KV"], ["KV"], 8)
    ts(T.BASE[:], T.KV[:, 0:144:18], 1.0, OP.add, None, None, ["KV"], ["BASE"], 8)
    ts(T.SX[:], T.SX[:], T.R16[:, 0:1], OP.add, None, None, ["R16", "SX"], ["SX"], 16)
    ts(T.E16[:], T.I16[:], T.R16[:, 0:1], OP.is_equal, None, None, ["R16", "I16"], ["E16"], 16)
    ts(T.TM[:], T.I16[:], T.R16[:, 0:1], OP.is_ge, -64.0, OP.mult, ["R16", "I16"], ["TM"], 16)
    for b in range(16): fill(T.PWR[:, b:b + 1], 2.0 ** -b, ("PWR", b), 1)
    tt(T.E16[:], T.E16[:], T.PWR[:], OP.mult, ["E16"] + [("PWR", b) for b in range(16)], ["E16"], 16)
    V(lambda q: q.tensor_reduce(T.PW[:], T.E16[:], AxisListType.X, OP.add), ["E16"], ["PW"], 16)
    ts(T.BTI[:], T.IOTA[:, 0:1280], T.PW[:, 0:1], OP.mult, -0.5 + 2.0 ** -13, OP.add, ["IOTA", "PW"], ["BTI"], 1280)
    ts(T.BTI[:], T.BTI[:], 1, OP.bitwise_and, None, None, ["BTI"], ["BTI"], 1280)
    ts(T.BT[:], T.BTI[:], 2.0, OP.mult, -1.0, OP.add, ["BTI"], ["BT"], 1280)
    ts(T.NID[:], T.IDN[:], -1.0, OP.mult, None, None, ["IDN"], ["NID"], 128, (), 0.5)
    ts(T.I128[:], T.IDN[:], 128.0, OP.mult, None, None, ["IDN"], ["I128"], 128, (), 0.5)
    act(T.RMC[:], RM, AF.Copy, RMK, ["RMC"], 2048, scale=16384.0)
    act(T.RMN[:], RM, AF.Copy, RMK, ["RMN"], 2048, scale=-1.0)
    ts(T.RMW[:], RM, T.WT[:, 0:1], OP.mult, None, None, RMK + ["WT"], ["RMW"], 2048, (), 0.5)
    ts(T.DH[:], T.DV[:], -0.5, OP.mult, None, None, ["DV"], ["DH"], 8)
    for j in range(8):
        ts(T.DG[:, 128 * j:128 * j + 128], T.IDN[:], T.DH[:, j:j + 1], OP.mult, None, None, ["IDN", "DH"], [("DG", j)], 128, (), 0.5)
    copy(T.MU0[:], T.M0[:], ["M0"], ["MU0"], 16)

    for t in range(4):
        ZI, MU = T["ZI%d" % t], T["MU%d" % t]
        zk, mk = "ZI%d" % t, "MU%d" % t
        if t:
            nw = len(topo.engines(core, nxt))
            op("", None, [zk + "s"], [zk], 0, (), ("zi%d" % t, nw, 3.0))
            op("", None, [mk + "s"], [mk], 0, (), ("mi%d" % t, nw, 3.0))
        for h in range(2):
            a = 128 * h
            copy(T.OU[:, a:a + 128], T.MC[:, 0:1024].indirect(MU[:, 8 * h:8 * h + 8]), ["MC", mk], [("OU", h)], 128, (), CG)
            act(T["G%d" % h][:], T.GL[:].indirect(MU[:, 8 * h:8 * h + 8]), AF.Copy, ["GL", mk], ["G%d" % h], 128, gather=True)
        copy(T.MF[:], MU[:], [mk], ["MF"], 16)
        for h in range(2):
            Zb, Xb, Eb = T["P%d" % h], T["P%d" % (2 + h)], T["P%d" % (6 + h)]
            AB, PB, KB, C = T["AB%d" % h], T["PB%d" % h], T["KB%d" % h], T["C%d" % h]
            KS, KU, vg, sg, T2, R0, G_ = [T[n + str(h)] for n in ("KS", "KU", "VG", "SG", "T2", "R0", "G")]
            a, b, ch, NA = 128 * h, 128 * h + 128, CHS[h], NAS[h]
            mm([(Zb[:, 0:128], T.IDN[:], ZI[:, a:b], True, True)], [zk, "IDN"], ["ZP%d" % h], 128, [h])
            n = 128 // ch
            for c in range(ch):
                lo, s0 = 32 * n * c, a + n * c
                gath(PB[:, 15 + lo:15 + lo + 32 * n:2], T.PR[:].indirect(T.OU[:, s0:s0 + n]), False, ["PR", ("OU", h)], [("PB", h, c)], 16 * n)
                gath(AB[:, 16 + lo:16 + lo + 32 * n:2], T.AD[:].indirect(T.OU[:, s0:s0 + n]), True, ["AD", ("OU", h)], [("AB", h, c)], 16 * n)
            pk, ak = [("PB", h, c) for c in range(ch)], [("AB", h, c) for c in range(ch)]
            copy(PB[:, 16:4112:32], PB[:, 15:4111:32], pk + ["PBz%d" % h], ["P0%d" % h], 128, (), 0.5)
            copy(PB[:, 47:4112:32], G_[:], ["G%d" % h, "P0%d" % h], pk, 128, (), 0.5)
            V(lambda q, KB=KB, AB=AB, PB=PB: q.tensor_tensor_scan(KB[:, ::-1], AB[:, 4111:15:-1], PB[:, 4111:15:-1], 0.0, OP.add, OP.max),
              pk + ak + ["P0%d" % h, "PBz%d" % h, "ABo%d" % h], ["KB%d" % h], 4096, (), 0.5)
            mm([(Eb[:, 0:128], T.IDN[:], KB[:, 1:4096:32], True, False), (Eb[:, 0:128], T.IDN[:], AB[:, 16:4112:32], False, True)],
               ["IDN", "KB%d" % h] + ak, ["E0%d" % h], 256, [6 + h])
            act(R0[:], Eb[:, 0:128], AF.Relu, ["E0%d" % h], ["R0%d" % h], 128, [6 + h])
            us = T["P%d" % (4 + h)][:, 384 * h:384 * h + 128]
            for k in range(16):
                if k % 4 == 0: lst = []
                lst.append((us, T.RM[:, k, :, :], KB[:, 2 * k + 1:4096:32], k == 0, False))
                lst.append((us, T.RMN[:, k, :, :], KB[:, 2 * k:4096:32] if k else R0[:], False, k == 15))
                if k % 4 == 3: mm(lst, RMK + ["RMN", "KB%d" % h, "R0%d" % h, ("UO", h, k)], [("US", h, k), ("UO", h, k - 4)], 8 * 128, [4 + h])
            zsrc, zkey = ZI[:, a:b], zk
            kpos = [2 * k - 1 if k else 0 for k in range(17)]
            for j in range(2):
                for B, bank, ks in ((T.P7, 7, range(17 - NA, 17 - NA + min(4, NA))), (T.P6, 6, range(17 - NA + min(4, NA), 17))):
                    if not ks: continue
                    lst = []
                    for i, k in enumerate(ks):
                        lst.append((B[:, 128 * i:128 * i + 128], T.IDN[:], zsrc, True, False))
                        lst.append((B[:, 128 * i:128 * i + 128], T.NID[:], KB[:, kpos[k]:4096:32], False, True))
                    mm(lst, ["IDN", "NID", zkey, "KB%d" % h], [("D", h, bank)], 128 * len(lst), [bank])
                    for i, k in enumerate(ks):
                        act(C[:, :, :, k + 1], B[:, 128 * i:128 * i + 128], AF.Sign, [("D", h, bank)], [("C", h, k + 1)], 128, [bank], bias=0.5)
                for k in range(17 - NA):
                    tt(C[:, :, :, k + 1], KB[:, kpos[k]:4096:32], Zb[:, 0:128], OP.is_le, ["KB%d" % h, "ZP%d" % h], [("C", h, k + 1)], 128, [h], 1.0)
                cp = Xb[:, 0:144]
                lst = [(cp, T.TH[:], T["BR0%d" % h][:], True, False)] + ([(cp, T.CST[:], T["BR1%d" % h][:], False, False)] if NA else [])
                lst += [(cp, T.RMC[:, r, :, :], C[:, :, r, :], False, r == 15) for r in range(16)]
                mm(lst, [("C", h, k) for k in range(18)] + [("BR", h)] + ["RMC", "CST", "TH"], ["CP%d" % h], 18 * 144, [2 + h])
                V(lambda q, KS=KS, cp=cp: q.tensor_tensor_scan(KS[:], cp, T.KV[:], 0.0, OP.max, OP.min), ["CP%d" % h, "KV"], ["KS%d" % h], 144, [2 + h])
                copy(KU[:], KS[:, 17:144:18], ["KS%d" % h], ["KU%d" % h], 8)
                abk = ak + ["ABo%d" % h, "KU%d" % h]
                act(sg[:], AB[:].indirect(KU[:]), AF.Sign, abk, ["SG%d" % h], 128, gather=True, bias=192.0)
                gath(vg[:], AB[:].indirect(KU[:]), False, abk, ["VG%d" % h], 128)
                xs, dj = Xb[:, 144:272], 2 * t + j
                mm([(xs, T.IDN[:], zsrc, True, False), (xs, T.NID[:], vg[:], False, False), (xs, T.I128[:], sg[:], False, True)],
                   [zkey, "IDN", "NID", "I128", "VG%d" % h, "SG%d" % h], ["X1%d" % h], 384, [2 + h])
                ts(T2[:], xs, 383.0, OP.min, 128.0, OP.subtract, ["X1%d" % h], ["T2%d" % h], 128, [2 + h])
                mm([(xs, T.IDN[:], T2[:], True, False), (xs, T.DG[:, 128 * dj:128 * dj + 128], sg[:], False, True)],
                   ["IDN", ("DG", dj), "T2%d" % h, "SG%d" % h], ["X1%d" % h], 256, [2 + h])
                bias, xr = T.DH[:, dj:dj + 1], ["X1%d" % h, "DH"]
                if j == 0: act(Zb[:, 0:128], xs, AF.Abs, xr, ["ZP%d" % h], 128, [h, 2 + h], bias=bias)
                act(T.Z[:, a:b], xs, AF.Abs, xr, ["Z%d" % h], 128, [2 + h], bias=bias)
                if t == 3 and j == 1: act(T.ZF[:, a:b], xs, AF.Abs, xr, ["ZF%d" % h], 128, [2 + h], bias=bias)
                zsrc, zkey = T.Z[:, a:b], "Z%d" % h
            ul = T.P2[:, 400 + 8 * h:408 + 8 * h]
            mm([(ul, T.RMW[:, r, :, :], T.Z[:, a + r:b:16], r == 0, r == 15) for r in range(16)], ["RMW", "Z%d" % h], [("UL", h)], 1024, [2])
            tt(T.KD[:, 8 * h:8 * h + 8], KS[:, 17:144:18], T.BASE[:], OP.subtract, ["KS%d" % h, "BASE"], [("KD", h)], 8)

        def send(q, src, name, sem):
            rid, pid, _ = topo.addr(nxt)
            q.remote_dma(T[name][:], src[:], T.sem[sem % "i"], T.sem[sem % "l"], pid, rid, topo.mask(core, nxt))
        n1, ne = t + 1, len(topo.engines(core, nxt))
        if t < 3:
            op("G", lambda q, n1=n1: send(q, T.Z, "ZI%d" % n1, "z%%s%d" % n1), ["Z0", "Z1"], ["ZI%ds" % n1], 0.5, (), ("zl%d" % n1, ne, 2.0))
        KDK, ULK = [("KD", 0), ("KD", 1)], [("UL", 0), ("UL", 1)]
        copy(T.OF[:], T.OU[:], [("OU", 0), ("OU", 1)], ["OF"], 256)
        for h in range(2):
            us, a, uk = T["P%d" % (4 + h)][:, 384 * h:384 * h + 128], 128 * h, [("US", h, k) for k in (3, 7, 11, 15)]
            ts(T.P4[:, 128 + a:256 + a], us, 254.0, OP.is_lt, None, None, uk, [("GG", h)], 128, [4, 5])
            ts(T.P5[:, a:a + 128], us, 254.0, OP.is_lt, T.C37[:, 0:1], OP.mult, uk + ["C37"], [("W0", h)], 128, [4, 5])
        tt(T.OG[:], T.OF[:], T.P4[:, 128:384], OP.mult, ["OF", ("GG", 0), ("GG", 1)], ["OG"], 256, [4], 1.0)
        tt(T.P5[:, 0:256], T.OF[:], T.P5[:, 0:256], OP.add, ["OF", ("W0", 0), ("W0", 1)], ["W1"], 256, [5], 1.0)
        ts(T.GO[:], T.KD[:], 31.0, OP.is_equal, None, None, KDK, ["GO"], 16)
        ts(T.NN[:], T.KD[:], 0.0, OP.is_lt, None, None, KDK, ["NN"], 16)
        tt(T.GN[:], T.GO[:], T.NN[:], OP.add, ["GO", "NN"], ["GN"], 16)
        ts(T.T36[:], T.GN[:], 36.0, OP.mult, 1.0, OP.add, ["GN"], ["T36"], 16)
        tt(T.BM[:], T.T36[:], T.MF[:], OP.mult, ["T36", "MF"], ["BM"], 16)
        ts(T.CA[:], T.GO[:], -1.0, OP.mult, 1.0, OP.add, ["GO"], ["CA"], 16)
        tt(T.CB[:], T.CA[:], T.SX[:], OP.mult, ["CA", "SX"], ["CB"], 16)
        UL = T.P2[:, 400:416]
        tt(T.UM[:], T.GN[:], UL, OP.mult, ULK + ["GN"], ["UM"], 16, [2])
        copy(T.UI[:], UL, ULK, ["UI"], 16, [2])
        tt(T.MI[:], T.UM[:], T.BM[:], OP.add, ["UM", "BM"], ["MI"], 16)
        ts(T.MI2[:], T.MI[:], 1023, OP.bitwise_and, None, None, ["MI"], ["MI2"], 16)
        if t < 3:
            copy(T.MS[:], T.MI2[:], ["MI2"], ["MS"], 16)
            op("G", lambda q, n1=n1: send(q, T.MS, "MU%d" % n1, "m%%s%d" % n1), ["MS"], ["MU%ds" % n1], 0.5, (), ("ml%d" % n1, ne, 2.0))
        else:
            copy(T.YM[:], T.MI2[:], ["MI2"], ["YM"], 16)
        tt(T.XA[:], T.MI2[:], T.GO[:], OP.mult, ["MI2", "GO"], ["XA"], 16)
        tt(T.X[:], T.XA[:], T.CB[:], OP.add, ["XA", "CB"], ["X"], 16)
        copy(T.XU[:], T.X[:], ["X"], ["XU"], 16)
        ts(T.UI2[:], T.UI[:], 4095, OP.bitwise_and, None, None, ["UI"], ["UI2"], 16)
        copy(T.UU[:], T.UI2[:], ["UI2"], ["UU"], 16)
        tt(T.DM[:], T.SX[:], T.X[:], OP.subtract, ["SX", "X"], ["DM"], 16)
        act(T.YB[:], T.BT[:].indirect(T.XU[:]), AF.Copy, ["BT", "XU"], ["YB"], 256, gather=True)
        for gg in range(8):
            if gg in (1, 4, 7): act(T.BD[:, :, gg, :], T.YB[:], AF.Copy, ["YB", "MSK"], [("BD", gg)], 256, scale=T.MSK[:, gg:gg + 1])
            else: ts(T.BD[:, :, gg, :], T.YB[:], T.MSK[:, gg:gg + 1], OP.mult, None, None, ["YB", "MSK"], [("BD", gg)], 256, (), 0.5)
        for cs, bank in (((14, 15), 1), ((12, 13), 3), ((10, 11), 0), ((7, 8, 9), 7), ((0, 1, 2, 3, 4, 5, 6), 6)):
            off, P, lst, red = 0, T["P%d" % bank], [], []
            for c in cs:
                lh, nn = T.BD[:, c, :, :], 16 * c + 16
                if c: lst.append((P[:, off:off + 16 * c], lh, T.YB[:, 0:16 * c], True, True))
                lst.append((P[:, off + 16 * c:off + nn], lh, T.YB[:, 16 * c:nn], True, False))
                lst.append((P[:, off + 16 * c:off + nn], T.IDN[:], T.TM[:], False, True))
                red.append((c, off, nn))
                off += nn
            mm(lst, [("BD", gg) for gg in range(8)] + ["YB", "IDN", "TM"], [("E", bank)], off + 100 * len(cs), [bank])
            for c, o, nn in red:
                if c < 10: V(lambda q, c=c, o=o, nn=nn, P=P: q.tensor_reduce(T.DVX[:, c:c + 1], P[:, o:o + nn], AxisListType.X, OP.max), [("E", bank)], [("DF", c)], nn, [bank])
                else: act(T.JK[:, 0:nn], P[:, o:o + nn], AF.Relu, [("E", bank)], ["JK", ("DF", c)], nn, [bank], bias=-15.0, accum_out=T.DA[:, c:c + 1])
        ts(T.DF[:, 0:10], T.DVX[:, 0:10], 15.5, OP.is_ge, None, None, [("DF", c) for c in range(10)], ["DF0"], 10)
        ts(T.DF[:, 10:16], T.DA[:, 10:16], 0.5, OP.is_ge, None, None, [("DF", c) for c in range(10, 16)], ["DF1"], 6)
        tt(T.XD[:], T.DF[:], T.DM[:], OP.mult, ["DF0", "DF1", "DM"], ["XD"], 16)
        tt(T.XF[:], T.XD[:], T.X[:], OP.add, ["XD", "X"], ["XF"], 16)
        copy(T.XFU[:], T.XF[:], ["XF"], ["XFU"], 16)
        V(lambda q: q.tensor_tensor(T.PP[:], T.IOTA[:].indirect(T.UU[:]), T.OG[:], OP.mult), ["IOTA", "UU", "OG"], ["PP"], 256, (), CG)
        ts(T.SS[:], T.PP[:], 5, OP.arith_shift_right, None, None, ["PP"], ["SS"], 256)
        tt(T.TT[:], T.SS[:], T.P5[:, 0:256], OP.add, ["SS", "W1"], ["TT"], 256, [5], 1.0)
        ts(T.NW[:], T.TT[:], 4095, OP.bitwise_and, None, None, ["TT"], ["NW"], 256)
        if t < 3:
            copy(T.MC[:].indirect(T.XFU[:]), T.NW[:], ["NW", "XFU"], ["MC"], 256, (), 3.8)
            ts(T.GOB[:], T.KD[:], 31.0, OP.is_equal, None, None, KDK, ["GOB"], 16)
            mm([(T.P7[:, 496:512], T.ON[:, 0:128], T.GOB[:], True, True)], ["ON", "GOB"], ["APS"], 64, [7])
            V(lambda q: q.tensor_reduce(T.AC[:], T.P7[:, 496:512], AxisListType.X, OP.add), ["APS"], ["AC"], 16, [7])
            copy(T.AI[:], T.AC[:], ["AC"], ["AI"], 1)
            ts(T.AP[:], T.AI[:], 1, OP.bitwise_and, None, None, ["AI"], ["AP"], 1)
            ts(T.AT[:], T.AP[:], -128.0, OP.mult, -1472.0, OP.add, ["AP"], ["AT"], 1)
            ts(T.TH[:], T.ON[:, 0:128], T.AT[:, 0:1], OP.mult, None, None, ["ON", "AT"], ["TH"], 128, (), 0.5)
        else:
            copy(T.MCF[:, 0:1024], T.MC[:, 0:1024], ["MC"], ["MCF"], 1024)
            copy(T.MCF[:].indirect(T.XFU[:]), T.NW[:], ["NW", "XFU"], ["MCF"], 256, (), 3.8)
            op("S", lambda q: q.dma_start(T.yz[:], T.ZF[:]), ["ZF0", "ZF1"], [], 0.1, (), ("so0", 16, 2))
            op("S", lambda q: q.dma_start(T.ym[:], T.YM[:]), ["YM"], [], 0.1, (), ("so1", 16, 2))
            op("S", lambda q: q.dma_start(T.ymc[:], T.MCF[:, 0:1024]), ["MCF"], [], 0.1, (), ("so2", 16, 4))
    return ops


def name_of(o):
    w = o["w"][0] if o["w"] else "out"
    if not isinstance(w, tuple): return w
    piece = w[0] in ("PB", "AB")
    return w[0] + (str(w[1]) if piece or w[0] in ("C", "OU", "US", "UL", "KD", "D") else "") + (str(w[2]) if piece else "")


def schedule(ops):
    off = {k: float(v) for k, v in (x.split("=") for x in OFF.split())}
    pin = dict(x.split("=") for x in PIN.split())
    n = len(ops)
    kids = [[] for _ in ops]
    need = [0] * n
    for i, o in enumerate(ops):
        for d in o["hard"] | o["soft"]:
            kids[d].append(i)
            need[i] += 1
    lat = [o["done"][2] if o["done"] else o["cost"] for o in ops]
    prio = [0.0] * n
    for i in range(n - 1, -1, -1):
        prio[i] = lat[i] + 0.08 + max([prio[k] for k in kids[i]] + [0.0])
    prio = [p + off.get(name_of(o), 0.0) for p, o in zip(prio, ops)]
    for o in ops:
        if len(o["eng"]) > 1: o["cand"] = pin.get(name_of(o), o["eng"])
        else: o["cand"] = o["eng"]
    free, fin, start, est = dict.fromkeys("VATGS", 0.0), [0.0] * n, [0.0] * n, [0.0] * n
    ready = [i for i in range(n) if need[i] == 0]
    order = []
    while ready:
        beg = []
        for i in ready:
            e = ops[i]["cand"]
            beg.append(est[i] if not e else max(est[i], free[e]) if len(e) == 1 else max(est[i], min(free["V"] + DV, free["A"])))
        m = min(beg) + EPS
        best = None
        for i, b in zip(ready, beg):
            if b <= m and (best is None or prio[i] > prio[best[0]]): best = (i, b)
        i, b = best
        o = ops[i]
        ready.remove(i)
        e = o["cand"]
        if len(e) > 1: e = "V" if free["V"] + DV <= free["A"] else "A"
        if len(o["eng"]) > 1: o["fn"] = (lambda f, e: lambda q: f(q, e))(o["fn"], e)
        o["eng"] = o["cand"] = e
        if e:
            b = max(est[i], free[e])
            free[e] = b + o["cost"]
        start[i], fin[i] = b, b + lat[i]
        order.append(i)
        for k in kids[i]:
            need[k] -= 1
            w = 0.06 if ops[k]["cand"] == e else WAKE
            est[k] = max(est[k], fin[i] + w if i in ops[k]["hard"] else start[i])
            if need[k] == 0: ready.append(k)
    return order, start, fin


def rank_program(g, core, T, topo):
    rank = T.rank_of(core)
    if rank is None:
        return
    nxt = T.cores[(rank + 1) % len(T.cores)]
    ops = build(T, topo, core, nxt)
    order, _, _ = schedule(ops)
    Q = {"V": g.vector, "A": g.scalar, "T": g.tensor, "G": g, "S": g.sync}
    cnt = {e: 0 for e in Q}
    done, know = {}, {}
    known = {e: {} for e in Q}
    for i in order:
        o = ops[i]
        e = o["eng"]
        if not e:
            done[i] = o["done"][:2]
            know[i] = {done[i][0]: done[i][1]}
            continue
        kn = known[e]
        wants = {}
        for d in o["hard"]:
            s, v = done[d]
            if kn.get(s, 0) < v and wants.get(s, (0, 0))[0] < v: wants[s] = (v, d)
        for s in sorted(wants, key=lambda s: -wants[s][1]):
            v, d = wants[s]
            if kn.get(s, 0) >= v: continue
            Q[e].wait_ge(T.sem[s], v)
            for a, b in know[d].items():
                if kn.get(a, 0) < b: kn[a] = b
        x = o["fn"](Q[e])
        if o["done"]:
            done[i] = o["done"][:2]
            if x is not None: x.then_inc(T.sem[done[i][0]], done[i][1])
        else:
            cnt[e] += 1
            done[i] = ("s" + e, cnt[e])
            x.then_inc(T.sem["s" + e], 1)
        know[i] = dict(kn)
        know[i][done[i][0]] = done[i][1]
    kn = known["S"]
    for i in reversed(order):
        s, v = done[i]
        if kn.get(s, 0) < v:
            g.sync.wait_ge(T.sem[s], v)
            kn[s] = v
